import numpy as np, ml_dtypes
CORES = [1,5,17,21,33,37,49,53]
N = 8
import mx_ref
BF = ml_dtypes.bfloat16
def gentries(a):
    return np.ascontiguousarray(a.reshape(8, 16, -1).transpose(0, 2, 1)).reshape(8, -1)
def gtable(e):
    e = np.asarray(e); return np.ascontiguousarray(e.reshape(8, -1, 16).transpose(0, 2, 1)).reshape(128, -1).astype(np.int32)
def gcols(t, e):
    v = np.concatenate([t.reshape(8, 16, -1, 4), np.zeros((8, 16, 1, 4), BF)], axis=2)
    return np.ascontiguousarray(np.stack([v[g][:, e[g]] for g in range(8)])).reshape(128, -1)
def gpick(z, e):
    return np.concatenate([z[16 * g:16 * g + 16][:, e[g]] for g in range(8)])
def tile(rs):
    return np.stack(rs, axis=2).reshape(128, -1).astype(BF)
def pick(q, e):
    c = np.concatenate([q[0].reshape(128, -1, 4), np.zeros((128, 1, 4), np.uint8)], axis=1); s = np.concatenate([q[1], np.ones((16, 1), np.uint8)], axis=1)
    return (np.ascontiguousarray(c[:, e].reshape(128, -1)), np.ascontiguousarray(s[:, e]))
def join(*qs):
    return (np.concatenate([q[0] for q in qs], axis=1), np.concatenate([q[1] for q in qs], axis=1))
def put(q, e, v):
    c, s = q[0].reshape(128, -1, 4).copy(), q[1].copy(); c[:, e] = v[0].reshape(128, -1, 4); s[:, e] = v[1]
    return (c.reshape(128, -1), s)
def pk(c, s):
    return (np.ascontiguousarray(c), mx_ref.live(s))
def emit(q):
    return q[0], q[1]
def packed(v, rng):
    q = [mx_ref.quantize(np.ascontiguousarray(v[r])) for r in range(N)]
    return np.stack([a for a, b in q]), np.stack([mx_ref.plane(b, rng) for a, b in q])
def values_of_codes():
    e, c = np.zeros((128, 128, 4), np.float32), np.zeros((128, 2, 4), np.uint8)
    e[np.arange(128), np.arange(128), 0] = 1
    c[:127, :, 0] = np.arange(256).reshape(2, 128).T[:127]
    return mx_ref.matmul(mx_ref.quantize(e.reshape(128, 512).astype(BF)), (c.reshape(128, 8), np.full((16, 2), 127, np.uint8))).T.reshape(-1).astype(np.float64)
CODE_VALUE, SCALE_VALUE = values_of_codes(), 2.0 ** (np.arange(256) - 127.0)
def decode(q):
    return (CODE_VALUE[q[0]].reshape(16, 8, -1, 4) * SCALE_VALUE[q[1]][:, None, :, None] + 0.0).reshape(128, -1).astype(np.float32)
def f(rng, *shape):
    return mx_ref.flush((rng.standard_normal(shape, dtype=np.float32) * np.exp2(rng.integers(-2, 3, shape[:-1] + (1,)))).astype(BF))
def wide(rng, *shape, cols=0):
    v = rng.standard_normal(shape, dtype=np.float32) * np.exp2(rng.integers(-12, 13, shape)).astype(np.float32)
    if cols: v *= np.repeat(np.exp2(rng.integers(-cols, cols + 1, shape[:-2] + (1, shape[-1] // 4))) * (rng.random(shape[:-2] + (1, shape[-1] // 4)) > 0.0625), 4, axis=-1).astype(np.float32)
    return mx_ref.flush(v.astype(BF))
C = 320
STEP = [1, 2, 4]
def numbers_of(rng):
    return {"x": np.array(f(rng, N, 128, 4 * C)), "u": np.array(f(rng, N, 128, 512)), "v": np.array(f(rng, N, 128, 512))}
def drawn(rng):
    e = np.tile(np.arange(C), (N, 8, 1))
    p, k, s, m = rng.permuted(e, axis=2), rng.permuted(e, axis=2), rng.permuted(e, axis=2), np.zeros_like(e)
    np.put_along_axis(m, s[:, :, ::2], s[:, :, 1::2], 2)
    np.put_along_axis(m, s[:, :, 1::2], s[:, :, ::2], 2)
    return p, k, m
def stored(p, k, m):
    return {"pg": np.stack([gtable(p[r]) for r in range(N)]), "kg": np.stack([gtable(k[r]) for r in range(N)]), "mg": np.stack([gtable(m[r]) for r in range(N)])}
def layers(rng):
    return np.array(f(rng, N, 128, 2048)).reshape(N, 8, 16, 4, 8, 16, 4)
def weights(rng, w):
    c, s = packed(np.ascontiguousarray(w).reshape(N, 128, 2048), rng)
    return {"wc": c, "ws": s}
def setup_inputs(rng):
    return {**numbers_of(rng), **stored(*drawn(rng)), **weights(rng, layers(rng))}
def setup_inputs_ties(rng):
    d = numbers_of(rng)
    o = rng.permutation(N)
    s = rng.integers(-1, 2, (N, 2, 8, C))
    s[o[0]] = 0
    s[o[1]] = 1
    s[o[2], 0] = np.where(np.arange(C) % 2 == 1, 1, rng.integers(-1, 1, (8, C)))
    x = d["x"].astype(np.float32).reshape(N, 8, 16, C, 4)
    u = d["u"].astype(np.float32).reshape(N, 128, 128, 4)
    for i in range(2):
        x[:, :, i] = 0
        x[:, :, i, :, 0] = s[:, i]
        u[:, :, i::16] = 0
        for h in range(0, 128, 16): u[:, h + i, h + i, 0] = 1
    p, k, m = drawn(rng)
    p[o[2]] = k[o[2]] = np.arange(C)
    m[o[2]] = np.arange(C) ^ 1
    w = layers(rng)
    w[:, :, :, :, :, :8] = 0
    return {"x": x.reshape(N, 128, 4 * C).astype(BF), "u": u.reshape(N, 128, 512).astype(BF), "v": d["v"], **stored(p, k, m), **weights(rng, w)}
def setup_inputs_near(rng):
    d = numbers_of(rng)
    o = rng.permutation(N)
    k = np.where(o % 2 == 0, 2.0 ** -30, 1.0)
    x = np.zeros((N, 8, 16, C, 4))
    s = rng.integers(-1, 2, (N, 2, 8, C)) * k[:, None, None, None]
    for i in range(2):
        x[:, :, 2 * i, :, 0] = 1.125 * s[:, i]
        x[:, :, 2 * i + 1, :, 0] = -1.25 * s[:, i]
    x[:, :, 9, :, 0] = rng.choice([-1.0, 1.0], (N, 8, C)) * 2.0 ** -17
    x[:, :, 10:] = rng.choice([-1.0, 1.0], (N, 8, 6, C, 4)) * (1 + 0.125 * rng.integers(0, 8, (N, 8, 6, C, 4))) * np.exp2(-12.0 - rng.integers(0, 4, (N, 8, 6, C, 4)))
    u = d["u"].astype(np.float32).reshape(N, 128, 128, 4)
    u[:, :, ::16] = 0
    u[:, :, 1::16] = 0
    w = layers(rng)
    w[:, :, :8] = 0
    w[:, :, :, :, :, :10] = 0
    for r in range(N):
        for g in rng.permutation(8)[:4]: x[r, g, 0, rng.integers(C), 0] = 2.0 ** 30 * rng.choice([-1.0, 1.0])
        if o[r] == 0:
            x[r, :, :8] = 0
            x[r, :, 0, :, 0] = 2.0 ** -30
        for g in range(8):
            h = 16 * g
            if o[r] == 0:
                u[r, h + 4, h, 0] = 2.0 ** -30
                u[r, h + 4, h + 1, 0] = -2.0 ** -30
                w[r, g, 8, 0, g, 4, 0] = 2.0 ** -8
                w[r, g, 9, 0, g, 4, 0] = 2.0 ** -22
            else:
                for i in range(2):
                    u[r, h + 2 * i, h + i, 0] = 1.125 * k[r]
                    u[r, h + 2 * i + 1, h + i, 0] = k[r]
    return {"x": x.astype(np.float32).reshape(N, 128, 4 * C).astype(BF), "u": u.reshape(N, 128, 512).astype(BF), "v": d["v"], **stored(*drawn(rng)), **weights(rng, w)}
def setup_inputs_odd(rng):
    d = numbers_of(rng)
    x = (1.0 + (2 * rng.integers(0, 64, (N, 16, 8, C, 4)) + 1) * 2.0 ** -7) * np.exp2(-rng.integers(0, 7, (N, 16, 8, C, 4)).astype(np.float64)) * rng.choice([-1.0, 1.0], (N, 16, 8, C, 4))
    x[:, ::2, 0, :, 0] = 1.96875 * 2.0 ** 8 * rng.choice([-1.0, 1.0], (8, 1))
    x[:, 1::2, 0, :, 0] = 1.96875 * 2.0 ** 8 * rng.choice([-1.0, 1.0], (N, 8, C))
    u = d["u"].astype(np.float32).reshape(N, 16, 8, 128, 4)
    u[:, :, 0, ::16] = 0
    u[:, :, :, 1::16] = 0
    h = rng.permutation(8) % 4
    for g in range(8):
        x[:, 2 * g, 1, :, 0] = (8 + rng.integers(0, 2, (N, C))) * 2.0 ** (int(h[g]) - 9)
        x[:, 2 * g, 2, :, 0] = -2.0 ** (int(h[g]) - 6)
        u[:, 2 * g, 1:3, 16 * g + 1, 0] = 1
    w = layers(rng)
    for i in (0, 8):
        w[:, :, i] = 0
        w[:, :, :, :, :, i] = 0
    w[:, :, :, 0, :, 1:3] = 0
    for g in range(8): w[:, g, 0, 0, g, 0, 0] = -0.5
    p, k, m = drawn(rng)
    t = int(rng.integers(N))
    p[t] = m[t] = np.arange(C)
    k[t] = rng.permutation(C)
    return {"x": x.astype(np.float32).reshape(N, 128, 4 * C).astype(BF), "u": u.reshape(N, 128, 512).astype(BF), "v": d["v"], **stored(p, k, m), **weights(rng, w)}
def setup_inputs_ends(rng):
    d = numbers_of(rng)
    o, ep, ek, em = [rng.permutation(N) % 4 for i in range(4)]
    s = rng.choice([-1.0, 1.0], (N, 128, C, 4))
    s[o == 0] = -1
    s[o == 1] = rng.choice([-1.0, 1.0], (N, 1, C, 1))[o == 1]
    x = s * (0.90 + 0.02 * rng.random((N, 128, C, 4))) * 2.0 ** 30
    tiny = (1 + 0.125 * rng.integers(0, 8, (N, 128, C, 4))) * 2.0 ** -30
    x[o == 3] = (s * tiny)[o == 3]
    x[:, 8:16] = tiny[:, 8:16]
    u = d["u"].astype(np.float32).reshape(N, 128, 128, 4)
    for r in range(N):
        h = rng.permutation(8)
        size = 2.0 ** -30 if o[r] == 3 else 2.0 ** 30
        u[r, :, ::16] = ((h % 2 * 2 - 1) * size)[None, :, None]
        u[r, :, 1::16] = ((h // 2 % 2 * 2 - 1) * size)[None, :, None]
    v = rng.choice([-1.0, 1.0], (N, 128, 512)) * np.where(o % 2 == 0, 2.0 ** 30, 2.0 ** -30)[:, None, None]
    p, k, m = drawn(rng)
    line = np.arange(C)
    p[ep == 0] = line
    p[ep == 1] = (line + 1) % C
    p[ep == 2] = C - 1 - line
    k[ek == 0] = line
    k[ek == 1] = C - 1 - line
    k[ek == 2] = (line + C - 1) % C
    m[em == 0] = line
    m[em == 1] = C - 1 - line
    m[em == 2] = line ^ 1
    w = np.zeros((N, 128, 4, 128, 4), np.float32)
    i = np.arange(128)
    for b in range(4): w[:, i, b, i, b] = np.where((i >= 8) & (i < 16), np.where(o == 3, 2.0 ** 8, 2.0 ** -8)[:, None], -0.25)
    return {"x": x.astype(np.float32).reshape(N, 128, 4 * C).astype(BF), "u": u.reshape(N, 128, 512).astype(BF), "v": v.astype(np.float32).astype(BF), **stored(p, k, m), **weights(rng, w.astype(BF))}
def setup_inputs_spread(rng):
    d = setup_inputs(rng)
    d["x"] = wide(rng, N, 128, 4 * C, cols=6)
    return d
def check_inputs(d):
    b = []
    for k in ("x", "u", "v"):
        a = np.abs(d[k].astype(np.float32))
        if not (np.isfinite(a).all() and ((a == 0) | (a >= 2.0 ** -30) & (a <= 2.0 ** 30)).all()): b.append("a value of " + k)
    none, least, most = [emit(mx_ref.quantize(np.full((128, 16), k, np.float32).astype(BF)))[1][0, 0] for k in (0.0, 2.0 ** -8, 2.0 ** 8)]
    top = emit(mx_ref.quantize(np.full((128, 16), 1.9921875, np.float32).astype(BF)))[0][0, 0] & 0x7F
    line = np.arange(C)
    for r in range(N):
        for k in ("pg", "kg"):
            if not (np.sort(gentries(d[k][r]), axis=1) == line).all(): b.append(k + ": no permutation")
        m = gentries(d["mg"][r])
        if not ((m >= 0) & (m < C)).all(): b.append("an entry of mg")
        elif not (np.take_along_axis(m, m, 1) == line).all(): b.append("mg: a mate's mate")
        if ((d["wc"][r] == 0x7F) | (d["wc"][r] == 0xFF)).any(): b.append("wc: a code that is no number")
        if ((d["wc"][r] & 0x7F) > top).any(): b.append("wc: a code that quantize_mx does not give")
        s = mx_ref.live(d["ws"][r])
        if ((s != none) & ((s < least) | (s > most))).any(): b.append("ws: a scale out of range")
    return b
def reference(x, u, v, pg, kg, mg, wc, ws):
    qu = [mx_ref.quantize(u[r]) for r in range(N)]
    lay = [pk(wc[r], ws[r]) for r in range(N)]
    p, k, m = [[gentries(a[r]).astype(np.int64) for r in range(N)] for a in (pg, kg, mg)]
    now = [x[r] for r in range(N)]
    for step in STEP:
        own, land, mosaic = [], [], []
        for r in range(N):
            q = mx_ref.quantize(now[r])
            s = mx_ref.matmul(qu[r], q)
            first = (s[::16] > 0).astype(np.int64)
            e = first + 2 * (s[1::16] > 0).astype(np.int64)
            at = np.zeros((8, C), np.int64)
            for g in range(8):
                power = np.ones(C, np.int64) if g == 0 else e[g - 1][at[g - 1]]
                a = k[r][g]
                for i in range(3): a = np.where(i < power, p[r][g][a], a)
                at[g] = a
            bit = np.take_along_axis(first, at, 1)
            p[r] = np.where(bit != np.take_along_axis(bit, m[r], 1), np.take_along_axis(p[r], m[r], 1), p[r])
            land.append(at)
            own.append(decode(q))
            mosaic.append(mx_ref.quantize(gcols(own[r].astype(BF), at)))
        made = []
        for r in range(N):
            h = [mx_ref.matmul(pick(lay[r], np.arange(128 * b, 128 * b + 128)), mosaic[r ^ step]) * np.float32(0.03125) for b in range(4)]
            made.append(tile([own[r][:, b::4] + gpick(h[b], land[r]) for b in range(4)]))
        now = made
    y, pl = np.zeros((N, 128, C), np.float32), np.zeros((N, 8, 2 * C), np.float32)
    oc, osc = np.zeros((N, 128, 4 * C), np.uint8), np.zeros((N, 16, C), np.uint8)
    for r in range(N):
        q = mx_ref.quantize(now[r])
        y[r] = mx_ref.matmul(mx_ref.quantize(v[r]), q)
        pl[r] = np.concatenate([land[r], p[r]], axis=1)
        oc[r], osc[r] = emit(q)
    return {"y": y, "pl": pl, "oc": oc, "osc": osc}

@@ -1,0 +1,436 @@
+import numpy as np
+from concourse.bass import DstId, RemoteDMATransfer
+from concourse.mybir import dt, AluOpType, AxisListType, ActivationFunctionType
+
+C = 320
+STEPS = [1, 2, 4]
+HALF = 160
+BLK = 112
+BIG = 1.0e29
+
+SCRATCH = {}
+SEMAPHORES = ["vs", "ss", "ts", "gs", "lsem"]
+
+
+def _sb(name, cols, d):
+    SCRATCH[name] = ("sbuf", [128, cols], d)
+
+
+for _k in range(4):
+    _sb("x%d" % _k, 4 * C, "bfloat16")
+    _sb("qx%d" % _k, C, "float8_e4m3fn_x4")
+    _sb("sx%d" % _k, C, "uint8")
+for _k in range(3):
+    _sb("rq%d" % _k, C, "float8_e4m3fn_x4")
+    _sb("rs%d" % _k, C, "uint8")
+    _sb("al%d" % _k, 20, "uint16")
+    _sb("rl%d" % _k, 20, "uint16")
+    SEMAPHORES += ["aq%d" % _k, "ar%d" % _k]
+for _k in range(2):
+    _sb("pw%d" % _k, C, "bfloat16")
+for _n, _c, _d in [
+    ("ut", 512, "bfloat16"), ("vt", 512, "bfloat16"), ("zt", 4 * C, "bfloat16"),
+    ("gt", 4 * 352, "bfloat16"), ("st", 600, "bfloat16"), ("kt", 576, "bfloat16"), ("et", 2048, "bfloat16"), ("rt", 2048, "bfloat16"),
+    ("pint", C, "int32"), ("kg32", 20, "int32"), ("mg32", 20, "int32"),
+    ("ip", 1, "int32"), ("ri", 1, "int32"), ("gi", 1, "int32"), ("oi", 1, "int32"),
+    ("rf", 1, "float32"), ("gf", 1, "float32"), ("of", 1, "float32"), ("zf", 1, "float32"), ("ef", 1, "float32"), ("sc", 8, "float32"),
+    ("i16c", C, "int32"), ("flat", C, "float32"), ("i20", 20, "int32"), ("iu", 24, "int32"),
+    ("jw", 20, "float32"), ("mj", 20, "float32"), ("jt", 20, "float32"), ("ro", 20, "uint16"), ("ml", 20, "uint16"), ("ul", 24, "uint16"),
+    ("dm", C, "bfloat16"), ("rm", C, "bfloat16"), ("mc", 8, "float32"), ("ident", 128, "bfloat16"),
+    ("oh", 16, "float32"), ("f1", 16, "float32"), ("f2", 16, "float32"), ("pr", 48, "float32"), ("al", 8, "float32"),
+    ("wa", 8, "float32"), ("cw", 12, "float32"), ("pc", 12, "float32"), ("co", 12, "float32"), ("cds", 4, "float32"), ("xc", 2, "float32"), ("gm", 16, "float32"),
+    ("tk", 24, "float32"), ("ti", 24, "int32"), ("wi", 24, "int32"), ("pd", 21, "int32"),
+    ("tb1", C, "float32"), ("tb", C, "bfloat16"), ("sg", C, "bfloat16"), ("vb", C, "bfloat16"), ("ym", C, "bfloat16"), ("ysc", C, "bfloat16"),
+    ("lm", C, "bfloat16"), ("lsc", C, "bfloat16"), ("lg", 80, "uint16"), ("lw", 80, "float32"),
+    ("ind", 80, "float32"), ("im", 80, "float32"), ("ia", 40, "float32"), ("af", 20, "float32"),
+    ("xb", 60, "float32"), ("df", 20, "float32"), ("sf", 40, "float32"), ("sl", 20, "uint16"),
+    ("fo", 4 * C, "bfloat16"), ("fp", 4 * C, "bfloat16"), ("hs", 4 * C, "float32"), ("yo", C, "float32"), ("plo", 2 * C, "float32"),
+]:
+    _sb(_n, _c, _d)
+for _n, _c in [("qu", 128), ("up", 384), ("qv", 128), ("wq", 512), ("qe", 512), ("qr", 512), ("qk", 144), ("qg", 352), ("qs", 150), ("qz", C)]:
+    _sb(_n, _c, "float8_e4m3fn_x4")
+    _sb(_n + "s", _c, "uint8")
+for _k in range(8):
+    SCRATCH["b%d" % _k] = ("psum", [128, 512], "float32")
+LOADS = ["dx", "du", "dp", "dk", "dm", "dw", "dws", "dv", "oy", "oc", "os", "op"]
+LOADS = ["d_" + _n for _n in LOADS]
+SEMAPHORES += LOADS
+
+A = AluOpType
+ACT = ActivationFunctionType
+
+
+def rank_program(g, core, T, topo):
+    rank = T.rank_of(core)
+    if rank is None:
+        return
+    queues = {"v": (g.vector, "vs"), "s": (g.scalar, "ss"), "t": (g.tensor, "ts"), "g": (g, "gs"), "y": (g.sync, None)}
+    cnt, seen, lastw, readers = {}, {}, {}, {}
+
+    def need(qn, reads, writes, free=()):
+        out = {}
+        for k in list(reads) + list(writes):
+            for s, v in lastw.get(k, []):
+                if k in writes and k in free:
+                    continue
+                out[s] = max(out.get(s, 0), v)
+        for k in writes:
+            for s, v in readers.get(k, []):
+                out[s] = max(out.get(s, 0), v)
+        for s, v in out.items():
+            if seen.get((qn, s), 0) < v:
+                queues[qn][0].wait_ge(T.sem[s], v)
+                seen[(qn, s)] = v
+
+    def done(reads, writes, s, v, free=()):
+        for k in reads:
+            readers.setdefault(k, []).append((s, v))
+        for k in writes:
+            if k in free:
+                lastw.setdefault(k, []).append((s, v))
+            else:
+                lastw[k] = [(s, v)]
+                readers[k] = []
+
+    def op(qn, fn, reads, writes, free=()):
+        need(qn, reads, writes, free)
+        s = queues[qn][1]
+        cnt[s] = cnt.get(s, 0) + 1
+        fn().then_inc(T.sem[s], 1)
+        done(reads, writes, s, cnt[s], free)
+
+    def dma(qn, s, out, in_, reads, writes, free=()):
+        need(qn, reads, writes, free)
+        cnt[s] = cnt.get(s, 0) + 16
+        queues[qn][0].dma_start(out, in_).then_inc(T.sem[s], 16)
+        done(reads, writes, s, cnt[s], free)
+
+    def V(fn, reads, writes, free=()):
+        op("v", fn, reads, writes, free)
+
+    def ts(out, i, s1, s2, *ops):
+        return lambda: g.vector.tensor_scalar(out, i, s1, s2, *ops)
+
+    def tt(out, a, b, o):
+        return lambda: g.vector.tensor_tensor(out, a, b, o)
+
+    def cp(out, i):
+        return lambda: g.vector.tensor_copy(out, i)
+
+    def ms(ap, c):
+        return lambda: g.vector.memset(ap, c)
+
+    def act(out, i, f, **kw):
+        return lambda: g.scalar.activation(out, i, f, **kw)
+
+    def quant(q, src, tiles, n):
+        V(lambda: g.vector.quantize_mx(T[q][:, 0:n], T[(q + "s") if q[:2] != "qx" else "sx" + q[2:]][:, 0:n], T[src][:, 0:4 * n]), tiles, [q])
+
+    def mm(bank, n, w, ws, wa, x, xs, xa, reads, start=True, stop=True):
+        op("t", lambda: g.tensor.matmul_mx(T[bank][:, 0:n], T[w][:, wa:wa + 128], T[ws][:, wa:wa + 128], T[x][:, xa:xa + n], T[xs][:, xa:xa + n], start, stop),
+           reads, [bank], [] if start else [bank])
+
+    dma("y", "d_dx", T.x0[:], T.x[:], [], ["x0"])
+    dma("s", "d_du", T.ut[:], T.u[:], [], ["ut"])
+    for r in range(16):
+        dma("y" if r % 2 else "s", "d_dp", T.pint[r::16, :], T.pg[:], [], ["pint"], ["pint"])
+    dma("s", "d_dk", T.kg32[:], T.kg[:], [], ["kg32"])
+    dma("y", "d_dm", T.mg32[:], T.mg[:], [], ["mg32"])
+    dma("y", "d_dw", T.wq[:].bitcast(dt.uint8), T.wc[:], [], ["wq"])
+    dma("y", "d_dws", T.wqs[:], T.ws[:], [], ["wqs"])
+    dma("y", "d_dv", T.vt[:], T.v[:], [], ["vt"])
+
+    op("g", lambda: g.iota(T.ip[:], [[0, 1]], 0, 1), [], ["ip"])
+    op("g", lambda: g.iota(T.iu[:], [[0, 3], [16, 8]], 0, 0), [], ["iu"])
+    op("g", lambda: g.iota(T.i20[:], [[1, 20]], 0, 0), [], ["i20"])
+    op("g", lambda: g.iota(T.i16c[:], [[0, 20], [1, 16]], 0, 0), [], ["i16c"])
+    op("g", lambda: g.iota(T.flat[:], [[1, C]], 0, 0, allow_small_or_imprecise_dtypes=True), [], ["flat"])
+
+    V(ts(T.ri[:], T.ip[:], 15, None, A.bitwise_and), ["ip"], ["ri"])
+    V(ts(T.gi[:], T.ip[:], 4, None, A.arith_shift_right), ["ip"], ["gi"])
+    V(cp(T.rf[:], T.ri[:]), ["ri"], ["rf"])
+    V(cp(T.gf[:], T.gi[:]), ["gi"], ["gf"])
+    pf, b10, b4, r20, hg, hf, ez = [T.sc[:, i:i + 1] for i in range(7)]
+    V(cp(pf, T.ip[:]), ["ip"], ["pf"])
+    V(ts(T.oi[:], T.gi[:], 1, None, A.bitwise_and), ["gi"], ["oi"])
+    V(ts(b10, T.rf[:], 10.0, None, A.is_ge), ["rf"], ["b10"])
+    V(ts(b4, T.rf[:], 4.0, None, A.is_ge), ["rf"], ["b4"])
+    V(ts(T.ul[:, 0:8], T.iu[:, 0:8], b10, None, A.add), ["iu", "b10"], ["ul0"])
+    V(ts(T.ul[:, 8:16], T.iu[:, 8:16], b4, None, A.add), ["iu", "b4"], ["ul1"])
+    V(cp(T.ul[:, 16:24], T.iu[:, 16:24]), ["iu"], ["ul2"])
+    V(ts(T.dm[:], T.i16c[:], T.rf[:, 0:1], None, A.is_equal), ["i16c", "rf"], ["dm"])
+    V(ts(T.rm[:], T.i16c[:], 1.0, None, A.min), ["i16c"], ["rm"])
+    V(ts(r20, T.rf[:], 20.0, None, A.mult), ["rf"], ["r20"])
+    V(ts(T.ro[:], T.i20[:], r20, None, A.add), ["i20", "r20"], ["ro"])
+    V(ts(T.jw[:], T.i20[:], 16.0, T.rf[:, 0:1], A.mult, A.add), ["i20", "rf"], ["jw"])
+    V(ts(T.ident[:], T.flat[:, 0:128], pf, None, A.is_equal), ["flat", "pf"], ["ident"])
+    V(ms(T.et[:], 0.0), [], ["etz"])
+
+    quant("qx0", "x0", ["x0"], C)
+    quant("qu", "ut", ["ut"], 128)
+    ULK = ["ul0", "ul1", "ul2"]
+    V(cp(T.up[:].bitcast(dt.uint32), T.qu[:].bitcast(dt.uint32).indirect(T.ul[:])), ["qu"] + ULK, ["up"])
+    op("s", act(T.ups[:], T.qus[:].indirect(T.ul[:]), ACT.Copy), ["qu"] + ULK, ["ups"])
+    for b in range(4):
+        op("s", act(T.et[:, 512 * b + b:512 * (b + 1):4], T.ident[:], ACT.Copy), ["ident", "etz"], ["et%d" % b])
+    ETK = ["et%d" % b for b in range(4)]
+    ETK.append("etz")
+
+    partner = [rank ^ s for s in STEPS]
+
+    def send(k, pairs, sem):
+        dst = T.cores[partner[k]]
+        rid, pid, _ = topo.addr(dst)
+        eng = topo.engines(core, dst)[:8]
+        m = sum(1 << e for e in eng)
+        for out, in_ in pairs:
+            g.remote_dma(out, in_, T.sem[sem], T.sem.lsem, pid, rid, m)
+            cnt["lsem"] = cnt.get("lsem", 0) + len(eng)
+            cnt[sem] = cnt.get(sem, 0) + len(eng)
+
+    def send_state(k):
+        need("g", ["qx%d" % k], [])
+        send(k, [(T["rq%d" % k][:].bitcast(dt.uint8), T["qx%d" % k][:].bitcast(dt.uint8)), (T["rs%d" % k][:], T["sx%d" % k][:])], "aq%d" % k)
+        done([], ["rq%d" % k], "aq%d" % k, cnt["aq%d" % k])
+
+    def send_list(k):
+        need("g", ["al%d" % k], [])
+        send(k, [(T["rl%d" % k][:], T["al%d" % k][:])], "ar%d" % k)
+        done([], ["rl%d" % k], "ar%d" % k, cnt["ar%d" % k])
+
+    def signs_mm(k):
+        q, s = "qx%d" % k, "sx%d" % k
+        mm("b0", C, "up", "ups", 0, q, s, 0, ["up", "ups", q])
+        mm("b1", C, "up", "ups", 128, q, s, 0, ["up", "ups", q])
+
+    def signs_table():
+        V(ts(T.tb1[:], T.b0[:, 0:C], 0.0, BIG, A.is_le, A.mult), ["b0"], ["tb1"])
+        V(tt(T.tb[:], T.b1[:, 0:C], T.tb1[:], A.is_gt), ["b1", "tb1"], ["tb"])
+
+    def unpack_mm(codes, scales, key):
+        for b in range(4):
+            mm("b%d" % (4 + b), C, "qe", "qes", 128 * b, codes, scales, 0, ["qe", key])
+
+    def unpack_copy(dst):
+        for b in range(4):
+            op("s", act(T[dst][:, C * b:C * (b + 1)], T["b%d" % (4 + b)][:, 0:C], ACT.Copy), ["b%d" % (4 + b)], ["%s%d" % (dst, b)])
+
+    send_state(0)
+    signs_mm(0)
+
+    for b in range(3):
+        V(cp(T.lg[:, 7 * b:7 * b + (7 if b < 2 else 6)], T.kg32[:, b::3]), ["kg32"], ["lg0%d" % b])
+    LG0 = ["lg00", "lg01", "lg02"]
+    V(ts(T.pw0[:], T.pint[:].indirect(T.ro[:]), -float(HALF), None, A.add), ["pint", "ro"], ["pw0"])
+
+    def candidates(n, k):
+        src = LG0 if n == 1 else ["lg%d" % (n - 1)]
+        pw = "pw%d" % (k % 2)
+        V(tt(T.lm[:], T[pw][:].indirect(T.lg[:, 20 * (n - 1):20 * n]), T.dm[:], A.mult), [pw, "dm"] + src, ["lm"])
+        V(lambda: g.vector.tensor_tensor_scan(T.lsc[:], T.rm[:], T.lm[:], 0.0, A.mult, A.add), ["rm", "lm"], ["lsc"])
+        V(ts(T.lg[:, 20 * n:20 * (n + 1)], T.lsc[:, 15::16], float(HALF), None, A.add), ["lsc"], ["lg%d" % n])
+        for b in range(3):
+            m = 7 if b < 2 else 6
+            o = 20 * n + 7 * b
+            V(cp(T.lw[:, 20 * n + b:20 * (n + 1):3], T.lg[:, o:o + m]), ["lg%d" % n], ["lw%d%d" % (n, b)])
+
+    candidates(1, 0)
+    candidates(2, 0)
+    signs_table()
+    V(ms(T.gt[:, 4 * C:], 0.0), [], ["gtz"])
+    candidates(3, 0)
+
+    def gather_signs():
+        for n in range(4):
+            rd = ["tb"] + (LG0 if n == 0 else ["lg%d" % n])
+            out, src = T.gt[:, n:4 * C:4], T.tb[:].indirect(T.lg[:, 20 * n:20 * (n + 1)])
+            if n in (0, 2):
+                V(cp(out, src), rd, ["gt%d" % n])
+            else:
+                op("s", act(out, src, ACT.Copy), rd, ["gt%d" % n])
+
+    def chain_constants():
+        V(cp(T.of[:], T.oi[:]), ["oi"], ["of"])
+        V(ts(T.zf[:], T.gf[:], 0.0, None, A.is_equal), ["gf"], ["zf"])
+        V(tt(ez, T.of[:], T.zf[:], A.add), ["of", "zf"], ["ez"])
+        V(ts(T.ef[:], ez, -1.0, 1.0, A.mult, A.add), ["ez"], ["ef"])
+        V(ts(T.oh[:], T.flat[:, 0:16], T.rf[:, 0:1], None, A.is_equal), ["flat", "rf"], ["oh"])
+        V(ms(T.f1[:], 0.0), [], ["f1"])
+        V(ms(T.f2[:], 0.0), [], ["f2"])
+        for col, val in ((0, 1.0), (4, 3.0), (10, 3.0)):
+            V(ms(T.f1[:, col:col + 1], val), [], ["f1"])
+        for col, val in ((0, 15.0), (4, 3840.0), (5, -15.0), (10, 240.0), (11, 15.0)):
+            V(ms(T.f2[:, col:col + 1], val), [], ["f2"])
+        V(tt(T.pr[:, 0:16], T.oh[:], T.f1[:], A.mult), ["oh", "f1"], ["pr0"])
+        V(tt(T.pr[:, 16:31], T.oh[:, 1:16], T.f1[:, 0:15], A.mult), ["oh", "f1"], ["pr1"])
+        V(tt(T.pr[:, 32:48], T.oh[:], T.f2[:], A.mult), ["oh", "f2"], ["pr2"])
+        for i, (lo, hi) in enumerate(((0, 16), (16, 31), (32, 48))):
+            V(lambda lo=lo, hi=hi, i=i: g.vector.tensor_reduce(T.al[:, i:i + 1], T.pr[:, lo:hi], AxisListType.X, A.add), ["pr%d" % i], ["alp%d" % i])
+        V(tt(T.al[:, 3:4], T.al[:, 0:1], T.zf[:], A.mult), ["alp0", "zf"], ["alp3"])
+        V(tt(T.al[:, 4:5], T.al[:, 0:1], T.ef[:], A.mult), ["alp0", "ef"], ["alp4"])
+        V(tt(T.al[:, 5:6], T.al[:, 1:2], T.ef[:], A.mult), ["alp1", "ef"], ["alp5"])
+        V(tt(T.al[:, 6:7], T.al[:, 2:3], T.of[:], A.mult), ["alp2", "of"], ["alp6"])
+        for i, val in enumerate((4096.0, 256.0, 16.0, 1.0, 8.0, 4.0, 2.0, 1.0)):
+            V(ms(T.wa[:, i:i + 1], val), [], ["wa%d" % i])
+        WA = ["wa%d" % i for i in range(8)]
+        V(ts(T.cw[:, 0:2], T.wa[:, 0:2], T.al[:, 4:5], None, A.mult), WA + ["alp4"], ["cw0"])
+        V(ts(T.cw[:, 2:4], T.wa[:, 2:4], T.al[:, 5:6], None, A.mult), WA + ["alp5"], ["cw1"])
+        V(ts(T.cw[:, 4:8], T.wa[:, 4:8], T.al[:, 6:7], None, A.mult), WA + ["alp6"], ["cw2"])
+        V(tt(T.cw[:, 8:12], T.cw[:, 0:4], T.cw[:, 4:8], A.add), ["cw0", "cw1", "cw2"], ["cw"])
+        V(tt(T.cw[:, 9:10], T.cw[:, 9:10], T.al[:, 3:4], A.add), ["cw", "alp3"], ["cw"])
+        V(ts(hg, T.gf[:], 4.0, 8.0, A.is_ge, A.mult), ["gf"], ["hg"])
+        V(tt(hf, hg, T.gf[:], A.add), ["hg", "gf"], ["hf"])
+        V(ts(T.gm[:], T.flat[:, 0:16], hf, None, A.is_equal), ["flat", "hf"], ["gm"])
+        V(ms(T.kt[:], 0.0), [], ["ktz"])
+        for n in range(4):
+            V(ts(T.kt[:, 32 + n:96 + n:4], T.gm[:], T.cw[:, 8 + n:9 + n], None, A.mult), ["gm", "cw", "ktz"], ["kt%d" % n])
+        quant("qk", "kt", ["ktz"] + ["kt%d" % n for n in range(4)], 144)
+        V(ms(T.tk[:], 4369.0), [], ["tk"])
+        V(ms(T.tk[:, 1:24:2], 15.0), [], ["tk"])
+        V(ms(T.tk[:, 0:12:4], 1.0), [], ["tk"])
+        V(ts(T.mc[:], T.flat[:, 0:8], T.gf[:, 0:1], None, A.is_equal), ["flat", "gf"], ["mc"])
+        V(ms(T.st[:], 0.0), [], ["stz"])
+        for i, val in enumerate((1.0, 2.0, 4.0, 8.0, 1.0, 16.0, 256.0, 4096.0)):
+            V(ms(T.pc[:, i:i + 1], val), [], ["pc%d" % i])
+        V(ms(T.pc[:, 8:12], -1.0), [], ["pc8"])
+        V(ms(T.pc[:, 9:10], 0.0), [], ["pc8"])
+        PC = ["pc%d" % i for i in range(9)]
+        for i, f in enumerate(("of", "ef", "zf")):
+            V(ts(T.co[:, 4 * i:4 * i + 4], T.pc[:, 4 * i:4 * i + 4], T[f][:, 0:1], None, A.mult), PC + [f], ["co%d" % i])
+        V(tt(T.cds[:], T.co[:, 0:4], T.co[:, 4:8], A.add), ["co0", "co1"], ["cds"])
+        V(tt(T.cds[:], T.cds[:], T.co[:, 8:12], A.add), ["cds", "co2"], ["cds"])
+        V(ts(T.xc[:, 0:1], T.of[:], 14.0, 2.0, A.mult, A.add), ["of"], ["xc0"])
+        V(ts(T.xc[:, 1:2], T.of[:], 4088.0, 8.0, A.mult, A.add), ["of"], ["xc1"])
+        V(cp(T.lw[:, 0:20], T.kg32[:]), ["kg32"], ["lw00"])
+        V(cp(T.ml[:], T.mg32[:]), ["mg32"], ["ml"])
+        V(cp(T.jt[:], T.mg32[:]), ["mg32"], ["jt"])
+        V(tt(T.mj[:], T.jt[:], T.jw[:], A.subtract), ["jt", "jw"], ["mj"])
+        quant("qr", "rt", RTK, 512)
+
+    V(ms(T.rt[:], 0.0), [], ["rtz"])
+    RTK = ["rtz"]
+    for own in range(2):
+        for gg in range(8):
+            to = gg + 1 - own
+            if to > 7:
+                continue
+            o = 1024 * own + 512 * (gg // 4) + 64 * to + gg % 4
+            key = "rt%d%d" % (own, gg)
+            op("s", act(T.rt[:, o:o + 61:4], T.dm[:, 0:16], ACT.Copy), ["dm", "rtz"], [key])
+            RTK.append(key)
+    quant("qe", "et", ETK, 512)
+    unpack_mm("qx0", "sx0", "qx0")
+    chain_constants()
+    quant("qv", "vt", ["vt"], 128)
+
+    LWK = ["lw00"] + ["lw%d%d" % (n, b) for n in range(1, 4) for b in range(3)]
+
+    def chain():
+        for b in range(3):
+            mm("b3", 128, "qg", "qgs", BLK * b, "qk", "qks", 8 - 4 * b, ["qg", "qk"], b == 0, b == 2)
+        V(tt(T.ti[:], T.b3[:, 0:24], T.tk[:], A.add), ["b3", "tk"], ["ti"])
+
+        def part(buf, gg):
+            o = 12 * (gg // 4) + gg % 4
+            return T[buf][:, o:12 * (gg // 4) + 12:4]
+
+        def spread(h):
+            for i in range(7):
+                m = 12 if i < 6 else 8
+                o = 88 * h + 12 * i
+                V(ts(T.st[:, o:o + m], T.wi[:, 12 * h:12 * h + m], T.mc[:, i:i + 1], None, A.mult),
+                  ["mc", "stz"] + ["wi%d" % q for q in range(4 * h, 4 * h + 4)], ["st%d%d" % (h, i)])
+
+        V(cp(part("wi", 0), part("ti", 0)), ["ti"], ["wi0"])
+        for gg in range(1, 8):
+            prev = part("ti", 0) if gg == 1 else part("wi", gg - 1)
+            V(tt(T.pd[:, 3 * (gg - 1):3 * gg], part("ti", gg), prev, A.mult), ["ti", "wi%d" % (gg - 1)], ["pd%d" % gg])
+            sh, mask = (3, 0x1111) if gg % 2 else (12, 15)
+            V(ts(part("wi", gg), T.pd[:, 3 * (gg - 1):3 * gg], sh, mask, A.arith_shift_right, A.bitwise_and), ["pd%d" % gg], ["wi%d" % gg])
+            if gg == 3:
+                pass
+        spread(0)
+        spread(1)
+        quant("qs", "st", ["stz"] + ["st%d%d" % (h, i) for h in range(2) for i in range(7)], 150)
+
+    def back(bank, own):
+        for h in range(2):
+            mm(bank, 128, "qr", "qrs", 256 * own + 128 * h, "qs", "qss", 22 * h, ["qr", "qs"], h == 0, h == 1)
+
+    def select(k):
+        for n in range(4):
+            V(ts(T.ind[:, 20 * n:20 * n + 20], T.b0[:, 0:20], T.cds[:, n:n + 1], None, A.is_equal), ["b0", "cds"], ["ind%d" % n])
+        V(tt(T.im[:], T.ind[:], T.lw[:], A.mult), ["ind%d" % n for n in range(4)] + LWK, ["im"])
+        V(tt(T.ia[:], T.im[:, 0:40], T.im[:, 40:80], A.add), ["im"], ["ia"])
+        V(tt(T.af[:], T.ia[:, 0:20], T.ia[:, 20:40], A.add), ["ia"], ["af"])
+        V(cp(T["al%d" % k][:], T.af[:]), ["af"], ["al%d" % k])
+
+    def exchange(k):
+        a = "al%d" % k
+        op("s", act(T.vb[:], T.sg[:].indirect(T[a][:]), ACT.Relu), ["sg", a], ["vb"])
+        V(ts(T.xb[:, 0:20], T.b1[:, 0:20], T.xc[:, 0:1], None, A.is_equal), ["b1", "xc0"], ["xb0"])
+        V(ts(T.xb[:, 20:40], T.b1[:, 0:20], T.xc[:, 1:2], None, A.is_equal), ["b1", "xc1"], ["xb1"])
+        V(tt(T.xb[:, 40:60], T.xb[:, 0:20], T.xb[:, 20:40], A.add), ["xb0", "xb1"], ["xb2"])
+        V(tt(T.ym[:], T.vb[:].indirect(T.ml[:]), T.dm[:], A.mult), ["vb", "ml", "dm"], ["ym"])
+        V(lambda: g.vector.tensor_tensor_scan(T.ysc[:], T.rm[:], T.ym[:], 0.0, A.mult, A.add), ["rm", "ym"], ["ysc"])
+        V(tt(T.df[:], T.ysc[:, 15::16], T.xb[:, 40:60], A.not_equal), ["ysc", "xb2"], ["df"])
+        V(tt(T.sf[:, 0:20], T.df[:], T.mj[:], A.mult), ["df", "mj"], ["sf0"])
+        V(tt(T.sf[:, 20:40], T.sf[:, 0:20], T.jw[:], A.add), ["sf0", "jw"], ["sf1"])
+        V(cp(T.sl[:], T.sf[:, 20:40]), ["sf1"], ["sl"])
+        old, new = "pw%d" % (k % 2), "pw%d" % (1 - k % 2)
+        op("s", act(T[new][:], T[old][:].indirect(T.sl[:]), ACT.Copy), [old, "sl"], [new])
+
+    for k in range(3):
+        qx, sx, last = "qx%d" % k, "sx%d" % k, k == 2
+        if k:
+            quant(qx, "x%d" % k, ["x%d_%d" % (k, b) for b in range(4)], C)
+            send_state(k)
+            signs_mm(k)
+            unpack_mm(qx, sx, qx)
+            candidates(3, k)
+            signs_table()
+        mm("b2", C, "up", "ups", 256, qx, sx, 0, ["up", "ups", qx])
+        gather_signs()
+        op("s", act(T.sg[:], T.b2[:, 0:C], ACT.Sign), ["b2"], ["sg"])
+        unpack_copy("fo")
+        quant("qg", "gt", ["gtz"] + ["gt%d" % n for n in range(4)], 352)
+        chain()
+        unpack_mm("rq%d" % k, "rs%d" % k, "rq%d" % k)
+        unpack_copy("fp")
+        back("b0", 0)
+        back("b1", 1)
+        select(k)
+        send_list(k)
+        exchange(k)
+        if not last:
+            candidates(1, k + 1)
+        for t in range(4):
+            out, src = T.zt[:, t:4 * C:4], T.fp[:, C * t:C * (t + 1)].indirect(T["rl%d" % k][:])
+            rd = ["fp%d" % t, "rl%d" % k]
+            if t % 2 == 0:
+                V(cp(out, src), rd, ["zt%d" % t])
+            else:
+                op("s", act(out, src, ACT.Copy), rd, ["zt%d" % t])
+        quant("qz", "zt", ["zt%d" % t for t in range(4)], C)
+        for b in range(4):
+            mm("b%d" % (4 + b), C, "wq", "wqs", 128 * b, "qz", "qzs", 0, ["wq", "wqs", "qz"])
+        for b in range(4):
+            op("s", act(T.hs[:, C * b:C * (b + 1)], T["b%d" % (4 + b)][:, 0:C], ACT.Copy, scale=0.03125), ["b%d" % (4 + b)], ["hs%d" % b])
+        if not last:
+            candidates(2, k + 1)
+        for b in range(4):
+            V(tt(T["x%d" % (k + 1)][:, b::4], T.hs[:, C * b:C * (b + 1)].indirect(T["al%d" % k][:]), T.fo[:, C * b:C * (b + 1)], A.add),
+              ["hs%d" % b, "al%d" % k, "fo%d" % b], ["x%d_%d" % (k + 1, b)])
+
+    op("s", act(T.plo[:, 0:C], T.flat[:].indirect(T.al2[:]), ACT.Copy), ["flat", "al2"], ["plo0"])
+    op("s", act(T.plo[:, C:2 * C], T.pw1[:], ACT.Copy, bias=float(HALF)), ["pw1"], ["plo1"])
+    quant("qx3", "x3", ["x3_%d" % b for b in range(4)], C)
+    mm("b0", C, "qv", "qvs", 0, "qx3", "sx3", 0, ["qv", "qx3"])
+    dma("y", "d_op", T.pl[:], T.plo[0::16, :], ["plo0", "plo1"], [])
+    dma("y", "d_oc", T.oc[:], T.qx3[:].bitcast(dt.uint8), ["qx3"], [])
+    for i in range(4):
+        dma("y", "d_os", T.osc[4 * i:4 * i + 4, :], T.sx3[32 * i:32 * i + 4, :], ["qx3"], [])
+    op("s", act(T.yo[:], T.b0[:, 0:C], ACT.Copy), ["b0"], ["yo"])
+    dma("s", "d_oy", T.y[:], T.yo[:], ["yo"], [])
+    for s, v in cnt.items():
+        g.wait_ge(T.sem[s], v)

@@ -7,6 +7,7 @@ STEPS = [1, 2, 4]
 HALF = 160
 BLK = 112
 BIG = 1.0e29
+TW = 172
 
 SCRATCH = {}
 SEMAPHORES = ["vs", "ss", "ts", "gs", "lsem"]
@@ -30,24 +31,23 @@ for _k in range(2):
     _sb("pw%d" % _k, C, "bfloat16")
 for _n, _c, _d in [
     ("ut", 512, "bfloat16"), ("vt", 512, "bfloat16"), ("zt", 4 * C, "bfloat16"),
-    ("gt", 4 * 352, "bfloat16"), ("st", 600, "bfloat16"), ("kt", 576, "bfloat16"), ("et", 2048, "bfloat16"), ("rt", 2048, "bfloat16"),
+    ("gt", 4 * 352, "bfloat16"), ("st", 600, "bfloat16"), ("kt", 720, "bfloat16"), ("et", 2048, "bfloat16"), ("rt", 2048, "bfloat16"),
     ("pint", C, "int32"), ("kg32", 20, "int32"), ("mg32", 20, "int32"),
-    ("ip", 1, "int32"), ("ri", 1, "int32"), ("gi", 1, "int32"), ("oi", 1, "int32"),
-    ("rf", 1, "float32"), ("gf", 1, "float32"), ("of", 1, "float32"), ("zf", 1, "float32"), ("ef", 1, "float32"), ("sc", 8, "float32"),
-    ("i16c", C, "int32"), ("flat", C, "float32"), ("i20", 20, "int32"), ("iu", 24, "int32"),
-    ("jw", 20, "float32"), ("mj", 20, "float32"), ("jt", 20, "float32"), ("ro", 20, "uint16"), ("ml", 20, "uint16"), ("ul", 24, "uint16"),
-    ("dm", C, "bfloat16"), ("rm", C, "bfloat16"), ("mc", 8, "float32"), ("ident", 128, "bfloat16"),
-    ("oh", 16, "float32"), ("f1", 16, "float32"), ("f2", 16, "float32"), ("pr", 48, "float32"), ("al", 8, "float32"),
-    ("wa", 8, "float32"), ("cw", 12, "float32"), ("pc", 12, "float32"), ("co", 12, "float32"), ("cds", 4, "float32"), ("xc", 2, "float32"), ("gm", 16, "float32"),
-    ("tk", 24, "float32"), ("ti", 24, "int32"), ("wi", 24, "int32"), ("pd", 21, "int32"),
+    ("ip", 1, "int32"), ("si", 4, "int32"), ("sc", 16, "float32"),
+    ("i16c", C, "bfloat16"), ("flat", C, "float32"), ("i20", 20, "int32"), ("iu", 24, "int32"), ("bt", 84, "float32"),
+    ("jw", 20, "float32"), ("mj", 20, "float32"), ("ro", 20, "uint16"), ("ml", 20, "uint16"), ("ul", 24, "uint16"),
+    ("dm", C, "bfloat16"), ("rm", C, "bfloat16"), ("mk", 84, "float32"), ("ident", 128, "bfloat16"),
+    ("oh", 48, "float32"), ("rw", 68, "float32"), ("pr", 48, "float32"), ("jk", 48, "float32"), ("al", 8, "float32"),
+    ("cw", 12, "float32"), ("co", 12, "float32"), ("cds", 4, "float32"), ("xc", 2, "float32"), ("gm", TW, "float32"),
+    ("tk", TW, "float32"), ("ti", TW, "int32"), ("pd", 147, "int32"),
     ("tb1", C, "float32"), ("tb", C, "bfloat16"), ("sg", C, "bfloat16"), ("vb", C, "bfloat16"), ("ym", C, "bfloat16"), ("ysc", C, "bfloat16"),
-    ("lm", C, "bfloat16"), ("lsc", C, "bfloat16"), ("lg", 80, "uint16"), ("lw", 80, "float32"),
+    ("lm", C, "bfloat16"), ("lsc", 3 * C, "bfloat16"), ("lg", 80, "uint16"), ("lw", 80, "float32"),
     ("ind", 80, "float32"), ("im", 80, "float32"), ("ia", 40, "float32"), ("af", 20, "float32"),
     ("xb", 60, "float32"), ("df", 20, "float32"), ("sf", 40, "float32"), ("sl", 20, "uint16"),
     ("fo", 4 * C, "bfloat16"), ("fp", 4 * C, "bfloat16"), ("hs", 4 * C, "float32"), ("yo", C, "float32"), ("plo", 2 * C, "float32"),
 ]:
     _sb(_n, _c, _d)
-for _n, _c in [("qu", 128), ("up", 384), ("qv", 128), ("wq", 512), ("qe", 512), ("qr", 512), ("qk", 144), ("qg", 352), ("qs", 150), ("qz", C)]:
+for _n, _c in [("qu", 128), ("up", 384), ("qv", 128), ("wq", 512), ("qe", 512), ("qr", 512), ("qk", 180), ("qg", 240), ("qh", 128), ("qs", 150), ("qz", C)]:
     _sb(_n, _c, "float8_e4m3fn_x4")
     _sb(_n + "s", _c, "uint8")
 for _k in range(8):
@@ -140,39 +140,77 @@ def rank_program(g, core, T, topo):
     dma("y", "d_dws", T.wqs[:], T.ws[:], [], ["wqs"])
     dma("y", "d_dv", T.vt[:], T.v[:], [], ["vt"])
 
-    op("g", lambda: g.iota(T.ip[:], [[0, 1]], 0, 1), [], ["ip"])
-    op("g", lambda: g.iota(T.iu[:], [[0, 3], [16, 8]], 0, 0), [], ["iu"])
-    op("g", lambda: g.iota(T.i20[:], [[1, 20]], 0, 0), [], ["i20"])
-    op("g", lambda: g.iota(T.i16c[:], [[0, 20], [1, 16]], 0, 0), [], ["i16c"])
-    op("g", lambda: g.iota(T.flat[:], [[1, C]], 0, 0, allow_small_or_imprecise_dtypes=True), [], ["flat"])
+    def iota(out, pattern, base, cm, reads, key):
+        op("g", lambda: g.iota(out, pattern, base, cm, allow_small_or_imprecise_dtypes=True), reads, [key])
 
-    V(ts(T.ri[:], T.ip[:], 15, None, A.bitwise_and), ["ip"], ["ri"])
-    V(ts(T.gi[:], T.ip[:], 4, None, A.arith_shift_right), ["ip"], ["gi"])
-    V(cp(T.rf[:], T.ri[:]), ["ri"], ["rf"])
-    V(cp(T.gf[:], T.gi[:]), ["gi"], ["gf"])
-    pf, b10, b4, r20, hg, hf, ez = [T.sc[:, i:i + 1] for i in range(7)]
-    V(cp(pf, T.ip[:]), ["ip"], ["pf"])
-    V(ts(T.oi[:], T.gi[:], 1, None, A.bitwise_and), ["gi"], ["oi"])
-    V(ts(b10, T.rf[:], 10.0, None, A.is_ge), ["rf"], ["b10"])
-    V(ts(b4, T.rf[:], 4.0, None, A.is_ge), ["rf"], ["b4"])
-    V(ts(T.ul[:, 0:8], T.iu[:, 0:8], b10, None, A.add), ["iu", "b10"], ["ul0"])
-    V(ts(T.ul[:, 8:16], T.iu[:, 8:16], b4, None, A.add), ["iu", "b4"], ["ul1"])
-    V(cp(T.ul[:, 16:24], T.iu[:, 16:24]), ["iu"], ["ul2"])
-    V(ts(T.dm[:], T.i16c[:], T.rf[:, 0:1], None, A.is_equal), ["i16c", "rf"], ["dm"])
-    V(ts(T.rm[:], T.i16c[:], 1.0, None, A.min), ["i16c"], ["rm"])
-    V(ts(r20, T.rf[:], 20.0, None, A.mult), ["rf"], ["r20"])
-    V(ts(T.ro[:], T.i20[:], r20, None, A.add), ["i20", "r20"], ["ro"])
-    V(ts(T.jw[:], T.i20[:], 16.0, T.rf[:, 0:1], A.mult, A.add), ["i20", "rf"], ["jw"])
-    V(ts(T.ident[:], T.flat[:, 0:128], pf, None, A.is_equal), ["flat", "pf"], ["ident"])
+    iota(T.ip[:], [[0, 1]], 0, 1, [], "ip")
+    iota(T.iu[:], [[0, 3], [16, 8]], 0, 0, [], "iu")
+    iota(T.flat[:], [[1, C]], 0, 0, [], "flat")
+    iota(T.i16c[:], [[0, 20], [1, 16]], 0, 0, [], "i16c")
+    iota(T.i20[:], [[1, 20]], 0, 0, [], "i20")
+    iota(T.jk[:], [[0, 3], [1, 16]], 0, 0, [], "jk")
+    iota(T.rw[:, 0:48], [[0, 48]], 0, 0, [], "rwz")
+    iota(T.rw[:, 48:62], [[0, 14]], 1, 0, [], "rwo")
+    iota(T.rw[:, 62:66], [[1, 4]], -1, 0, [], "rwp")
+    RWA, RWB = ["rwz"], ["rwo", "rwp"]
+    for col, val in ((0, 1), (4, 3), (10, 3), (17, 1), (21, 3), (27, 3), (32, 15), (36, 3840), (37, -15), (42, 240), (43, 15)):
+        iota(T.rw[:, col:col + 1], [[0, 1]], val, 0, ["rwz"], "rw%d" % col)
+        RWA.append("rw%d" % col)
+    for col, val in ((49, 2), (50, 4), (51, 8), (52, 4), (53, 2), (56, 16), (57, 256), (58, 4096), (59, 256), (60, 16)):
+        iota(T.rw[:, col:col + 1], [[0, 1]], val, 0, ["rwo"], "rw%d" % col)
+        RWB.append("rw%d" % col)
+    iota(T.bt[:], [[0, 7], [1, 12]], 0, 0, [], "bt")
+    iota(T.gm[:, 84:88], [[0, 4]], 0, 0, [], "gmz")
+
     V(ms(T.et[:], 0.0), [], ["etz"])
+    one = {n: T.sc[:, i:i + 1] for i, n in enumerate(("rf", "gf", "of", "pf", "b10", "b4", "r20", "zf", "e1", "ef", "h1", "h2", "hf", "g4"))}
+    V(ts(T.si[:, 0:1], T.ip[:], 15, None, A.bitwise_and), ["ip"], ["si0"])
+    V(ts(T.si[:, 1:2], T.ip[:], 4, None, A.arith_shift_right), ["ip"], ["si1"])
+    V(cp(one["pf"], T.ip[:]), ["ip"], ["pf"])
+    V(ts(T.si[:, 2:3], T.si[:, 1:2], 1, None, A.bitwise_and), ["si1"], ["si2"])
+    V(cp(T.sc[:, 0:3], T.si[:, 0:3]), ["si0", "si1", "si2"], ["rf"])
+    V(ts(one["b10"], one["rf"], 10.0, None, A.is_ge), ["rf"], ["b10"])
+    V(ts(one["b4"], one["rf"], 4.0, None, A.is_ge), ["rf"], ["b4"])
+    V(ts(one["r20"], one["rf"], 20.0, None, A.mult), ["rf"], ["r20"])
+    V(cp(T.ul[:, 16:24], T.iu[:, 16:24]), ["iu"], ["ul2"])
+    V(ts(T.ul[:, 0:8], T.iu[:, 0:8], one["b10"], None, A.add), ["iu", "b10"], ["ul0"])
+    V(ts(T.ul[:, 8:16], T.iu[:, 8:16], one["b4"], None, A.add), ["iu", "b4"], ["ul1"])
+    V(ts(T.ident[:], T.flat[:, 0:128], one["pf"], None, A.is_equal), ["flat", "pf"], ["ident"])
+    V(ts(T.dm[:], T.i16c[:], one["rf"], None, A.is_equal), ["i16c", "rf"], ["dm"])
+    V(ts(T.rm[:], T.i16c[:], 1.0, None, A.min), ["i16c"], ["rm"])
+    V(ts(T.ro[:], T.i20[:], one["r20"], None, A.add), ["i20", "r20"], ["ro"])
+
+    def S(out, i, f, reads, key, **kw):
+        op("s", act(out, i, f, **kw), reads, [key])
+
+    S(T.kt[:], T.et[:, 0:720], ACT.Copy, ["etz"], "ktz")
+    S(one["zf"], one["gf"], ACT.Relu, ["rf"], "zf", scale=-1.0, bias=1.0)
+    S(one["h1"], one["gf"], ACT.Relu, ["rf"], "h1", bias=-3.0)
+    S(one["g4"], one["gf"], ACT.Identity, ["rf"], "g4", bias=-4.0)
+    S(one["e1"], one["zf"], ACT.Identity, ["zf"], "e1", scale=-1.0, bias=1.0)
+    S(one["h2"], one["h1"], ACT.Sign, ["h1"], "h2")
+    S(one["ef"], one["of"], ACT.Identity, ["rf", "e1"], "ef", scale=-1.0, bias=one["e1"])
+    S(one["hf"], one["h2"], ACT.Identity, ["rf", "h2"], "hf", scale=8.0, bias=one["gf"])
+
+    S(T.gt[:, 4 * C:], T.et[:, 0:128], ACT.Copy, ["etz"], "gtz")
+    S(T.st[:], T.et[:, 0:600], ACT.Copy, ["etz"], "stz")
 
     quant("qx0", "x0", ["x0"], C)
     quant("qu", "ut", ["ut"], 128)
     ULK = ["ul0", "ul1", "ul2"]
     V(cp(T.up[:].bitcast(dt.uint32), T.qu[:].bitcast(dt.uint32).indirect(T.ul[:])), ["qu"] + ULK, ["up"])
     op("s", act(T.ups[:], T.qus[:].indirect(T.ul[:]), ACT.Copy), ["qu"] + ULK, ["ups"])
+    V(ts(T.oh[:], T.jk[:], one["rf"], None, A.is_equal), ["jk", "rf"], ["oh"])
+    V(tt(T.pr[:], T.oh[:], T.rw[:, 0:48], A.mult), ["oh"] + RWA, ["pr"])
+    for i in range(3):
+        S(T.jk[:, 16 * i:16 * i + 16], T.pr[:, 16 * i:16 * i + 16], ACT.Copy, ["pr", "oh"], "alp%d" % i, accum_out=T.al[:, i:i + 1])
+    for i, (src, f) in enumerate(((0, "zf"), (0, "ef"), (1, "ef"), (2, "of"))):
+        S(T.al[:, 3 + i:4 + i], T.al[:, src:src + 1], ACT.Copy, ["alp%d" % src, "rf" if f == "of" else f], "alp%d" % (3 + i), scale=one[f])
+    S(T.cw[:, 0:2], T.rw[:, 58:60], ACT.Copy, RWB + ["alp4"], "cw0", scale=T.al[:, 4:5])
+    S(T.cw[:, 2:4], T.rw[:, 60:62], ACT.Copy, RWB + ["alp5"], "cw1", scale=T.al[:, 5:6])
+    S(T.cw[:, 4:8], T.rw[:, 51:55], ACT.Copy, RWB + ["alp6"], "cw2", scale=T.al[:, 6:7])
     for b in range(4):
-        op("s", act(T.et[:, 512 * b + b:512 * (b + 1):4], T.ident[:], ACT.Copy), ["ident", "etz"], ["et%d" % b])
+        S(T.et[:, 512 * b + b:512 * (b + 1):4], T.ident[:], ACT.Copy, ["ident", "etz", "ktz", "stz", "gtz"], "et%d" % b)
     ETK = ["et%d" % b for b in range(4)]
     ETK.append("etz")
 
@@ -227,17 +265,30 @@ def rank_program(g, core, T, topo):
         src = LG0 if n == 1 else ["lg%d" % (n - 1)]
         pw = "pw%d" % (k % 2)
         V(tt(T.lm[:], T[pw][:].indirect(T.lg[:, 20 * (n - 1):20 * n]), T.dm[:], A.mult), [pw, "dm"] + src, ["lm"])
-        V(lambda: g.vector.tensor_tensor_scan(T.lsc[:], T.rm[:], T.lm[:], 0.0, A.mult, A.add), ["rm", "lm"], ["lsc"])
-        V(ts(T.lg[:, 20 * n:20 * (n + 1)], T.lsc[:, 15::16], float(HALF), None, A.add), ["lsc"], ["lg%d" % n])
+        lo, hi = C * (n - 1), C * n
+        V(lambda: g.vector.tensor_tensor_scan(T.lsc[:, lo:hi], T.rm[:], T.lm[:], 0.0, A.mult, A.add), ["rm", "lm"], ["lsc%d" % n])
+        V(ts(T.lg[:, 20 * n:20 * (n + 1)], T.lsc[:, lo + 15:hi:16], float(HALF), None, A.add), ["lsc%d" % n], ["lg%d" % n])
+
+    def candidates_own(n):
+        lo, hi = C * (n - 1), C * n
         for b in range(3):
-            m = 7 if b < 2 else 6
-            o = 20 * n + 7 * b
-            V(cp(T.lw[:, 20 * n + b:20 * (n + 1):3], T.lg[:, o:o + m]), ["lg%d" % n], ["lw%d%d" % (n, b)])
+            S(T.lw[:, 20 * n + b:20 * (n + 1):3], T.lsc[:, lo + 112 * b + 15:min(hi, lo + 112 * (b + 1)):16], ACT.Identity, ["lsc%d" % n], "lw%d%d" % (n, b), bias=float(HALF))
 
     candidates(1, 0)
+    candidates_own(1)
+    V(tt(T.cw[:, 8:12], T.cw[:, 0:4], T.cw[:, 4:8], A.add), ["cw0", "cw1", "cw2"], ["cw"])
+    V(ts(T.gm[:, 0:84], T.bt[:], one["hf"], None, A.is_equal), ["bt", "hf"], ["gm0"])
+    V(ts(T.gm[:, 88:172], T.bt[:], one["g4"], None, A.is_equal), ["bt", "g4"], ["gm1"])
+    V(tt(T.cw[:, 9:10], T.cw[:, 9:10], T.al[:, 3:4], A.add), ["cw", "alp3"], ["cw"])
+    for n in range(4):
+        S(T.kt[:, 32 + n:32 + 4 * TW:4], T.gm[:], ACT.Copy, ["gm0", "gm1", "gmz", "cw", "ktz"], "kt%d" % n, scale=T.cw[:, 8 + n:9 + n])
+    for i, (lo, f) in enumerate(((48, "of"), (55, "ef"), (62, "zf"))):
+        S(T.co[:, 4 * i:4 * i + 4], T.rw[:, lo:lo + 4], ACT.Copy, RWB + ["rf" if f == "of" else f], "co%d" % i, scale=one[f])
+    S(T.xc[:, 0:1], one["of"], ACT.Copy, ["rf"], "xc0", scale=14.0, bias=2.0)
+    S(T.xc[:, 1:2], one["of"], ACT.Copy, ["rf"], "xc1", scale=4088.0, bias=8.0)
     candidates(2, 0)
+    candidates_own(2)
     signs_table()
-    V(ms(T.gt[:, 4 * C:], 0.0), [], ["gtz"])
     candidates(3, 0)
 
     def gather_signs():
@@ -249,109 +300,61 @@ def rank_program(g, core, T, topo):
             else:
                 op("s", act(out, src, ACT.Copy), rd, ["gt%d" % n])
 
-    def chain_constants():
-        V(cp(T.of[:], T.oi[:]), ["oi"], ["of"])
-        V(ts(T.zf[:], T.gf[:], 0.0, None, A.is_equal), ["gf"], ["zf"])
-        V(tt(ez, T.of[:], T.zf[:], A.add), ["of", "zf"], ["ez"])
-        V(ts(T.ef[:], ez, -1.0, 1.0, A.mult, A.add), ["ez"], ["ef"])
-        V(ts(T.oh[:], T.flat[:, 0:16], T.rf[:, 0:1], None, A.is_equal), ["flat", "rf"], ["oh"])
-        V(ms(T.f1[:], 0.0), [], ["f1"])
-        V(ms(T.f2[:], 0.0), [], ["f2"])
-        for col, val in ((0, 1.0), (4, 3.0), (10, 3.0)):
-            V(ms(T.f1[:, col:col + 1], val), [], ["f1"])
-        for col, val in ((0, 15.0), (4, 3840.0), (5, -15.0), (10, 240.0), (11, 15.0)):
-            V(ms(T.f2[:, col:col + 1], val), [], ["f2"])
-        V(tt(T.pr[:, 0:16], T.oh[:], T.f1[:], A.mult), ["oh", "f1"], ["pr0"])
-        V(tt(T.pr[:, 16:31], T.oh[:, 1:16], T.f1[:, 0:15], A.mult), ["oh", "f1"], ["pr1"])
-        V(tt(T.pr[:, 32:48], T.oh[:], T.f2[:], A.mult), ["oh", "f2"], ["pr2"])
-        for i, (lo, hi) in enumerate(((0, 16), (16, 31), (32, 48))):
-            V(lambda lo=lo, hi=hi, i=i: g.vector.tensor_reduce(T.al[:, i:i + 1], T.pr[:, lo:hi], AxisListType.X, A.add), ["pr%d" % i], ["alp%d" % i])
-        V(tt(T.al[:, 3:4], T.al[:, 0:1], T.zf[:], A.mult), ["alp0", "zf"], ["alp3"])
-        V(tt(T.al[:, 4:5], T.al[:, 0:1], T.ef[:], A.mult), ["alp0", "ef"], ["alp4"])
-        V(tt(T.al[:, 5:6], T.al[:, 1:2], T.ef[:], A.mult), ["alp1", "ef"], ["alp5"])
-        V(tt(T.al[:, 6:7], T.al[:, 2:3], T.of[:], A.mult), ["alp2", "of"], ["alp6"])
-        for i, val in enumerate((4096.0, 256.0, 16.0, 1.0, 8.0, 4.0, 2.0, 1.0)):
-            V(ms(T.wa[:, i:i + 1], val), [], ["wa%d" % i])
-        WA = ["wa%d" % i for i in range(8)]
-        V(ts(T.cw[:, 0:2], T.wa[:, 0:2], T.al[:, 4:5], None, A.mult), WA + ["alp4"], ["cw0"])
-        V(ts(T.cw[:, 2:4], T.wa[:, 2:4], T.al[:, 5:6], None, A.mult), WA + ["alp5"], ["cw1"])
-        V(ts(T.cw[:, 4:8], T.wa[:, 4:8], T.al[:, 6:7], None, A.mult), WA + ["alp6"], ["cw2"])
-        V(tt(T.cw[:, 8:12], T.cw[:, 0:4], T.cw[:, 4:8], A.add), ["cw0", "cw1", "cw2"], ["cw"])
-        V(tt(T.cw[:, 9:10], T.cw[:, 9:10], T.al[:, 3:4], A.add), ["cw", "alp3"], ["cw"])
-        V(ts(hg, T.gf[:], 4.0, 8.0, A.is_ge, A.mult), ["gf"], ["hg"])
-        V(tt(hf, hg, T.gf[:], A.add), ["hg", "gf"], ["hf"])
-        V(ts(T.gm[:], T.flat[:, 0:16], hf, None, A.is_equal), ["flat", "hf"], ["gm"])
-        V(ms(T.kt[:], 0.0), [], ["ktz"])
-        for n in range(4):
-            V(ts(T.kt[:, 32 + n:96 + n:4], T.gm[:], T.cw[:, 8 + n:9 + n], None, A.mult), ["gm", "cw", "ktz"], ["kt%d" % n])
-        quant("qk", "kt", ["ktz"] + ["kt%d" % n for n in range(4)], 144)
-        V(ms(T.tk[:], 4369.0), [], ["tk"])
-        V(ms(T.tk[:, 1:24:2], 15.0), [], ["tk"])
-        V(ms(T.tk[:, 0:12:4], 1.0), [], ["tk"])
-        V(ts(T.mc[:], T.flat[:, 0:8], T.gf[:, 0:1], None, A.is_equal), ["flat", "gf"], ["mc"])
-        V(ms(T.st[:], 0.0), [], ["stz"])
-        for i, val in enumerate((1.0, 2.0, 4.0, 8.0, 1.0, 16.0, 256.0, 4096.0)):
-            V(ms(T.pc[:, i:i + 1], val), [], ["pc%d" % i])
-        V(ms(T.pc[:, 8:12], -1.0), [], ["pc8"])
-        V(ms(T.pc[:, 9:10], 0.0), [], ["pc8"])
-        PC = ["pc%d" % i for i in range(9)]
-        for i, f in enumerate(("of", "ef", "zf")):
-            V(ts(T.co[:, 4 * i:4 * i + 4], T.pc[:, 4 * i:4 * i + 4], T[f][:, 0:1], None, A.mult), PC + [f], ["co%d" % i])
-        V(tt(T.cds[:], T.co[:, 0:4], T.co[:, 4:8], A.add), ["co0", "co1"], ["cds"])
-        V(tt(T.cds[:], T.cds[:], T.co[:, 8:12], A.add), ["cds", "co2"], ["cds"])
-        V(ts(T.xc[:, 0:1], T.of[:], 14.0, 2.0, A.mult, A.add), ["of"], ["xc0"])
-        V(ts(T.xc[:, 1:2], T.of[:], 4088.0, 8.0, A.mult, A.add), ["of"], ["xc1"])
-        V(cp(T.lw[:, 0:20], T.kg32[:]), ["kg32"], ["lw00"])
-        V(cp(T.ml[:], T.mg32[:]), ["mg32"], ["ml"])
-        V(cp(T.jt[:], T.mg32[:]), ["mg32"], ["jt"])
-        V(tt(T.mj[:], T.jt[:], T.jw[:], A.subtract), ["jt", "jw"], ["mj"])
-        quant("qr", "rt", RTK, 512)
-
-    V(ms(T.rt[:], 0.0), [], ["rtz"])
-    RTK = ["rtz"]
-    for own in range(2):
-        for gg in range(8):
-            to = gg + 1 - own
-            if to > 7:
-                continue
-            o = 1024 * own + 512 * (gg // 4) + 64 * to + gg % 4
-            key = "rt%d%d" % (own, gg)
-            op("s", act(T.rt[:, o:o + 61:4], T.dm[:, 0:16], ACT.Copy), ["dm", "rtz"], [key])
-            RTK.append(key)
-    quant("qe", "et", ETK, 512)
-    unpack_mm("qx0", "sx0", "qx0")
-    chain_constants()
-    quant("qv", "vt", ["vt"], 128)
-
+    iota(T.tk[:], [[0, TW]], 4369, 0, [], "tka")
+    op("g", lambda: g.affine_select(T.tk[:], T.tk[:], [[0, TW // 2], [1, 2]], A.not_equal, 15.0, -1, 0), ["tka"], ["tkb"])
+    iota(T.tk[:, 0:84:4], [[0, 21]], 1, 0, ["tkb"], "tk")
+    iota(T.mk[:], [[1, 7], [0, 12]], 0, 0, [], "mka")
+    iota(T.mk[:, 80:84], [[0, 4]], -1, 0, ["mka"], "mkb")
+    iota(T.rt[:], [[0, 2048]], 0, 0, [], "rtz")
+    quant("qk", "kt", ["ktz"] + ["kt%d" % n for n in range(4)], 180)
     LWK = ["lw00"] + ["lw%d%d" % (n, b) for n in range(1, 4) for b in range(3)]
 
-    def chain():
+    def constants_a():
+        quant("qe", "et", ETK, 512)
+        V(ts(T.mk[:], T.mk[:], one["gf"], None, A.is_equal), ["mkb", "rf"], ["mk"])
+        unpack_mm("qx0", "sx0", "qx0")
+
+    def constants_b():
+        keys = ["rtz"]
+        for own in range(2):
+            for gg in range(8):
+                to = gg + 1 - own
+                if to > 7:
+                    continue
+                o = 1024 * own + 512 * (gg // 4) + 64 * to + gg % 4
+                keys.append("rt%d%d" % (own, gg))
+                S(T.rt[:, o:o + 61:4], T.dm[:, 0:16], ACT.Copy, ["dm", "rtz"], keys[-1])
+        V(tt(T.cds[:], T.co[:, 0:4], T.co[:, 4:8], A.add), ["co0", "co1"], ["cdh"])
+        V(tt(T.cds[:], T.cds[:], T.co[:, 8:12], A.add), ["cdh", "co2"], ["cds"])
+        quant("qr", "rt", keys, 512)
+
+    def part(gg):
+        return T.ti[:, 88 * (gg // 4) + gg % 4:88 * (gg // 4) + 84:4]
+
+    def chain(first):
         for b in range(3):
-            mm("b3", 128, "qg", "qgs", BLK * b, "qk", "qks", 8 - 4 * b, ["qg", "qk"], b == 0, b == 2)
-        V(tt(T.ti[:], T.b3[:, 0:24], T.tk[:], A.add), ["b3", "tk"], ["ti"])
-
-        def part(buf, gg):
-            o = 12 * (gg // 4) + gg % 4
-            return T[buf][:, o:12 * (gg // 4) + 12:4]
-
-        def spread(h):
-            for i in range(7):
-                m = 12 if i < 6 else 8
-                o = 88 * h + 12 * i
-                V(ts(T.st[:, o:o + m], T.wi[:, 12 * h:12 * h + m], T.mc[:, i:i + 1], None, A.mult),
-                  ["mc", "stz"] + ["wi%d" % q for q in range(4 * h, 4 * h + 4)], ["st%d%d" % (h, i)])
-
-        V(cp(part("wi", 0), part("ti", 0)), ["ti"], ["wi0"])
+            q = "qg" if b < 2 else "qh"
+            mm("b3", TW, q, q + "s", BLK * (b % 2), "qk", "qks", 8 - 4 * b, [q, "qk"], b == 0, b == 2)
+        if first:
+            constants_a()
+        V(tt(T.ti[:], T.b3[:, 0:TW], T.tk[:], A.add), ["b3", "tk"], ["ti"] + ["ti%d" % q for q in range(8)])
         for gg in range(1, 8):
-            prev = part("ti", 0) if gg == 1 else part("wi", gg - 1)
-            V(tt(T.pd[:, 3 * (gg - 1):3 * gg], part("ti", gg), prev, A.mult), ["ti", "wi%d" % (gg - 1)], ["pd%d" % gg])
+            pd = T.pd[:, 21 * (gg - 1):21 * gg]
+            V(tt(pd, part(gg), part(gg - 1), A.mult), ["ti%d" % gg, "ti%d" % (gg - 1)], ["pd%d" % gg])
             sh, mask = (3, 0x1111) if gg % 2 else (12, 15)
-            V(ts(part("wi", gg), T.pd[:, 3 * (gg - 1):3 * gg], sh, mask, A.arith_shift_right, A.bitwise_and), ["pd%d" % gg], ["wi%d" % gg])
-            if gg == 3:
-                pass
-        spread(0)
-        spread(1)
-        quant("qs", "st", ["stz"] + ["st%d%d" % (h, i) for h in range(2) for i in range(7)], 150)
+            V(ts(part(gg), pd, sh, mask, A.arith_shift_right, A.bitwise_and), ["pd%d" % gg], ["ti%d" % gg])
+            if gg % 4 == 3:
+                o = 88 * (gg // 4)
+                V(tt(T.st[:, o:o + 84], T.ti[:, o:o + 84], T.mk[:], A.mult), ["mk", "stz"] + ["ti%d" % q for q in range(gg - 3, gg + 1)], ["st%d" % gg])
+        if first:
+            constants_b()
+        quant("qs", "st", ["stz", "st3", "st7"], 150)
+        if first:
+            V(cp(T.lw[:, 0:20], T.kg32[:]), ["kg32"], ["lw00"])
+            V(ts(T.jw[:], T.i20[:], 16.0, one["rf"], A.mult, A.add), ["i20", "rf"], ["jw"])
+            V(cp(T.ml[:], T.mg32[:]), ["mg32"], ["ml"])
+            V(tt(T.mj[:], T.mg32[:], T.jw[:], A.subtract), ["mg32", "jw"], ["mj"])
+            unpack_copy("fo")
 
     def back(bank, own):
         for h in range(2):
@@ -391,10 +394,13 @@ def rank_program(g, core, T, topo):
             signs_table()
         mm("b2", C, "up", "ups", 256, qx, sx, 0, ["up", "ups", qx])
         gather_signs()
+        candidates_own(3)
         op("s", act(T.sg[:], T.b2[:, 0:C], ACT.Sign), ["b2"], ["sg"])
-        unpack_copy("fo")
-        quant("qg", "gt", ["gtz"] + ["gt%d" % n for n in range(4)], 352)
-        chain()
+        if k:
+            unpack_copy("fo")
+        for q, lo, hi in (("qg", 0, 240), ("qh", 224, 352)):
+            V(lambda q=q, lo=lo, hi=hi: g.vector.quantize_mx(T[q][:], T[q + "s"][:], T.gt[:, 4 * lo:4 * hi]), ["gtz"] + ["gt%d" % n for n in range(4)], [q])
+        chain(k == 0)
         unpack_mm("rq%d" % k, "rs%d" % k, "rq%d" % k)
         unpack_copy("fp")
         back("b0", 0)
@@ -407,10 +413,12 @@ def rank_program(g, core, T, topo):
         for t in range(4):
             out, src = T.zt[:, t:4 * C:4], T.fp[:, C * t:C * (t + 1)].indirect(T["rl%d" % k][:])
             rd = ["fp%d" % t, "rl%d" % k]
-            if t % 2 == 0:
+            if t == 0:
                 V(cp(out, src), rd, ["zt%d" % t])
             else:
                 op("s", act(out, src, ACT.Copy), rd, ["zt%d" % t])
+        if not last:
+            candidates_own(1)
         quant("qz", "zt", ["zt%d" % t for t in range(4)], C)
         for b in range(4):
             mm("b%d" % (4 + b), C, "wq", "wqs", 128 * b, "qz", "qzs", 0, ["wq", "wqs", "qz"])
@@ -418,19 +426,23 @@ def rank_program(g, core, T, topo):
             op("s", act(T.hs[:, C * b:C * (b + 1)], T["b%d" % (4 + b)][:, 0:C], ACT.Copy, scale=0.03125), ["b%d" % (4 + b)], ["hs%d" % b])
         if not last:
             candidates(2, k + 1)
+            candidates_own(2)
         for b in range(4):
             V(tt(T["x%d" % (k + 1)][:, b::4], T.hs[:, C * b:C * (b + 1)].indirect(T["al%d" % k][:]), T.fo[:, C * b:C * (b + 1)], A.add),
               ["hs%d" % b, "al%d" % k, "fo%d" % b], ["x%d_%d" % (k + 1, b)])
 
+    quant("qv", "vt", ["vt"], 128)
     op("s", act(T.plo[:, 0:C], T.flat[:].indirect(T.al2[:]), ACT.Copy), ["flat", "al2"], ["plo0"])
     op("s", act(T.plo[:, C:2 * C], T.pw1[:], ACT.Copy, bias=float(HALF)), ["pw1"], ["plo1"])
     quant("qx3", "x3", ["x3_%d" % b for b in range(4)], C)
-    mm("b0", C, "qv", "qvs", 0, "qx3", "sx3", 0, ["qv", "qx3"])
+    for h in range(2):
+        mm("b%d" % h, C // 2, "qv", "qvs", 0, "qx3", "sx3", C // 2 * h, ["qv", "qx3"])
     dma("y", "d_op", T.pl[:], T.plo[0::16, :], ["plo0", "plo1"], [])
     dma("y", "d_oc", T.oc[:], T.qx3[:].bitcast(dt.uint8), ["qx3"], [])
     for i in range(4):
         dma("y", "d_os", T.osc[4 * i:4 * i + 4, :], T.sx3[32 * i:32 * i + 4, :], ["qx3"], [])
-    op("s", act(T.yo[:], T.b0[:, 0:C], ACT.Copy), ["b0"], ["yo"])
-    dma("s", "d_oy", T.y[:], T.yo[:], ["yo"], [])
+    V(cp(T.yo[:, 0:C // 2], T.b0[:, 0:C // 2]), ["b0"], ["yo0"])
+    op("s", act(T.yo[:, C // 2:C], T.b1[:, 0:C // 2], ACT.Copy), ["b1"], ["yo1"])
+    dma("s", "d_oy", T.y[:], T.yo[:], ["yo0", "yo1"], [])
     for s, v in cnt.items():
         g.wait_ge(T.sem[s], v)

import numpy as np
from concourse.bass import DstId, RemoteDMATransfer
from concourse.mybir import dt, AluOpType, AxisListType, ActivationFunctionType

C = 320
STEPS = [1, 2, 4]
HALF = 160
BLK = 112
BIG = 1.0e29
TW = 172

SCRATCH = {}
SEMAPHORES = ["vs", "ss", "ts", "gs", "lsem"]


def _sb(name, cols, d):
    SCRATCH[name] = ("sbuf", [128, cols], d)


for _k in range(4):
    _sb("x%d" % _k, 4 * C, "bfloat16")
    _sb("qx%d" % _k, C, "float8_e4m3fn_x4")
    _sb("sx%d" % _k, C, "uint8")
for _k in range(3):
    _sb("rq%d" % _k, C, "float8_e4m3fn_x4")
    _sb("rs%d" % _k, C, "uint8")
    _sb("al%d" % _k, 20, "uint16")
    _sb("rl%d" % _k, 20, "uint16")
    SEMAPHORES += ["aq%d" % _k, "ar%d" % _k]
for _k in range(2):
    _sb("pw%d" % _k, C, "bfloat16")
for _n, _c, _d in [
    ("ut", 512, "bfloat16"), ("vt", 512, "bfloat16"), ("zt", 4 * C, "bfloat16"),
    ("gt", 4 * 352, "bfloat16"), ("st", 600, "bfloat16"), ("kt", 720, "bfloat16"), ("et", 2048, "bfloat16"), ("rt", 2048, "bfloat16"),
    ("pint", C, "int32"), ("kg32", 20, "int32"), ("mg32", 20, "int32"),
    ("ip", 1, "int32"), ("si", 4, "int32"), ("sc", 16, "float32"),
    ("i16c", C, "bfloat16"), ("flat", C, "float32"), ("i20", 20, "int32"), ("iu", 24, "int32"), ("bt", 84, "float32"),
    ("jw", 20, "float32"), ("mj", 20, "float32"), ("ro", 20, "uint16"), ("ml", 20, "uint16"), ("ul", 24, "uint16"),
    ("dm", C, "bfloat16"), ("rm", C, "bfloat16"), ("mk", 84, "float32"), ("ident", 128, "bfloat16"),
    ("oh", 48, "float32"), ("rw", 68, "float32"), ("pr", 48, "float32"), ("jk", 48, "float32"), ("al", 8, "float32"),
    ("cw", 12, "float32"), ("co", 12, "float32"), ("cds", 4, "float32"), ("xc", 2, "float32"), ("gm", TW, "float32"),
    ("tk", TW, "float32"), ("ti", TW, "int32"), ("pd", 147, "int32"),
    ("tb1", C, "float32"), ("tb", C, "bfloat16"), ("sg", C, "bfloat16"), ("vb", C, "bfloat16"), ("ym", C, "bfloat16"), ("ysc", C, "bfloat16"),
    ("lm", C, "bfloat16"), ("lsc", 3 * C, "bfloat16"), ("lg", 80, "uint16"), ("lw", 80, "float32"),
    ("ind", 80, "float32"), ("im", 80, "float32"), ("ia", 40, "float32"), ("af", 20, "float32"),
    ("xb", 60, "float32"), ("df", 20, "float32"), ("sf", 40, "float32"), ("sl", 20, "uint16"),
    ("fo", 4 * C, "bfloat16"), ("fp", 4 * C, "bfloat16"), ("hs", 4 * C, "float32"), ("yo", C, "float32"), ("plo", 2 * C, "float32"),
]:
    _sb(_n, _c, _d)
for _n, _c in [("qu", 128), ("up", 384), ("qv", 128), ("wq", 512), ("qe", 512), ("qr", 512), ("qk", 180), ("qg", 240), ("qh", 128), ("qs", 150), ("qz", C)]:
    _sb(_n, _c, "float8_e4m3fn_x4")
    _sb(_n + "s", _c, "uint8")
for _k in range(8):
    SCRATCH["b%d" % _k] = ("psum", [128, 512], "float32")
LOADS = ["dx", "du", "dp", "dk", "dm", "dw", "dws", "dv", "oy", "oc", "os", "op"]
LOADS = ["d_" + _n for _n in LOADS]
SEMAPHORES += LOADS

A = AluOpType
ACT = ActivationFunctionType


def rank_program(g, core, T, topo):
    rank = T.rank_of(core)
    if rank is None:
        return
    queues = {"v": (g.vector, "vs"), "s": (g.scalar, "ss"), "t": (g.tensor, "ts"), "g": (g, "gs"), "y": (g.sync, None)}
    cnt, seen, lastw, readers = {}, {}, {}, {}

    def need(qn, reads, writes, free=()):
        out = {}
        for k in list(reads) + list(writes):
            for s, v in lastw.get(k, []):
                if k in writes and k in free:
                    continue
                out[s] = max(out.get(s, 0), v)
        for k in writes:
            for s, v in readers.get(k, []):
                out[s] = max(out.get(s, 0), v)
        for s, v in out.items():
            if seen.get((qn, s), 0) < v:
                queues[qn][0].wait_ge(T.sem[s], v)
                seen[(qn, s)] = v

    def done(reads, writes, s, v, free=()):
        for k in reads:
            readers.setdefault(k, []).append((s, v))
        for k in writes:
            if k in free:
                lastw.setdefault(k, []).append((s, v))
            else:
                lastw[k] = [(s, v)]
                readers[k] = []

    def op(qn, fn, reads, writes, free=()):
        need(qn, reads, writes, free)
        s = queues[qn][1]
        cnt[s] = cnt.get(s, 0) + 1
        fn().then_inc(T.sem[s], 1)
        done(reads, writes, s, cnt[s], free)

    def dma(qn, s, out, in_, reads, writes, free=()):
        need(qn, reads, writes, free)
        cnt[s] = cnt.get(s, 0) + 16
        queues[qn][0].dma_start(out, in_).then_inc(T.sem[s], 16)
        done(reads, writes, s, cnt[s], free)

    def V(fn, reads, writes, free=()):
        op("v", fn, reads, writes, free)

    def ts(out, i, s1, s2, *ops):
        return lambda: g.vector.tensor_scalar(out, i, s1, s2, *ops)

    def tt(out, a, b, o):
        return lambda: g.vector.tensor_tensor(out, a, b, o)

    def cp(out, i):
        return lambda: g.vector.tensor_copy(out, i)

    def ms(ap, c):
        return lambda: g.vector.memset(ap, c)

    def act(out, i, f, **kw):
        return lambda: g.scalar.activation(out, i, f, **kw)

    def quant(q, src, tiles, n):
        V(lambda: g.vector.quantize_mx(T[q][:, 0:n], T[(q + "s") if q[:2] != "qx" else "sx" + q[2:]][:, 0:n], T[src][:, 0:4 * n]), tiles, [q])

    def mm(bank, n, w, ws, wa, x, xs, xa, reads, start=True, stop=True):
        op("t", lambda: g.tensor.matmul_mx(T[bank][:, 0:n], T[w][:, wa:wa + 128], T[ws][:, wa:wa + 128], T[x][:, xa:xa + n], T[xs][:, xa:xa + n], start, stop),
           reads, [bank], [] if start else [bank])

    dma("y", "d_dx", T.x0[:], T.x[:], [], ["x0"])
    dma("s", "d_du", T.ut[:], T.u[:], [], ["ut"])
    for r in range(16):
        dma("y" if r % 2 else "s", "d_dp", T.pint[r::16, :], T.pg[:], [], ["pint"], ["pint"])
    dma("s", "d_dk", T.kg32[:], T.kg[:], [], ["kg32"])
    dma("y", "d_dm", T.mg32[:], T.mg[:], [], ["mg32"])
    dma("y", "d_dw", T.wq[:].bitcast(dt.uint8), T.wc[:], [], ["wq"])
    dma("y", "d_dws", T.wqs[:], T.ws[:], [], ["wqs"])
    dma("y", "d_dv", T.vt[:], T.v[:], [], ["vt"])

    def iota(out, pattern, base, cm, reads, key):
        op("g", lambda: g.iota(out, pattern, base, cm, allow_small_or_imprecise_dtypes=True), reads, [key])

    iota(T.ip[:], [[0, 1]], 0, 1, [], "ip")
    iota(T.iu[:], [[0, 3], [16, 8]], 0, 0, [], "iu")
    iota(T.flat[:], [[1, C]], 0, 0, [], "flat")
    iota(T.i16c[:], [[0, 20], [1, 16]], 0, 0, [], "i16c")
    iota(T.i20[:], [[1, 20]], 0, 0, [], "i20")
    iota(T.jk[:], [[0, 3], [1, 16]], 0, 0, [], "jk")
    iota(T.rw[:, 0:48], [[0, 48]], 0, 0, [], "rwz")
    iota(T.rw[:, 48:62], [[0, 14]], 1, 0, [], "rwo")
    iota(T.rw[:, 62:66], [[1, 4]], -1, 0, [], "rwp")
    RWA, RWB = ["rwz"], ["rwo", "rwp"]
    for col, val in ((0, 1), (4, 3), (10, 3), (17, 1), (21, 3), (27, 3), (32, 15), (36, 3840), (37, -15), (42, 240), (43, 15)):
        iota(T.rw[:, col:col + 1], [[0, 1]], val, 0, ["rwz"], "rw%d" % col)
        RWA.append("rw%d" % col)
    for col, val in ((49, 2), (50, 4), (51, 8), (52, 4), (53, 2), (56, 16), (57, 256), (58, 4096), (59, 256), (60, 16)):
        iota(T.rw[:, col:col + 1], [[0, 1]], val, 0, ["rwo"], "rw%d" % col)
        RWB.append("rw%d" % col)
    iota(T.bt[:], [[0, 7], [1, 12]], 0, 0, [], "bt")
    iota(T.gm[:, 84:88], [[0, 4]], 0, 0, [], "gmz")

    V(ms(T.et[:], 0.0), [], ["etz"])
    one = {n: T.sc[:, i:i + 1] for i, n in enumerate(("rf", "gf", "of", "pf", "b10", "b4", "r20", "zf", "e1", "ef", "h1", "h2", "hf", "g4"))}
    V(ts(T.si[:, 0:1], T.ip[:], 15, None, A.bitwise_and), ["ip"], ["si0"])
    V(ts(T.si[:, 1:2], T.ip[:], 4, None, A.arith_shift_right), ["ip"], ["si1"])
    V(cp(one["pf"], T.ip[:]), ["ip"], ["pf"])
    V(ts(T.si[:, 2:3], T.si[:, 1:2], 1, None, A.bitwise_and), ["si1"], ["si2"])
    V(cp(T.sc[:, 0:3], T.si[:, 0:3]), ["si0", "si1", "si2"], ["rf"])
    V(ts(one["b10"], one["rf"], 10.0, None, A.is_ge), ["rf"], ["b10"])
    V(ts(one["b4"], one["rf"], 4.0, None, A.is_ge), ["rf"], ["b4"])
    V(ts(one["r20"], one["rf"], 20.0, None, A.mult), ["rf"], ["r20"])
    V(cp(T.ul[:, 16:24], T.iu[:, 16:24]), ["iu"], ["ul2"])
    V(ts(T.ul[:, 0:8], T.iu[:, 0:8], one["b10"], None, A.add), ["iu", "b10"], ["ul0"])
    V(ts(T.ul[:, 8:16], T.iu[:, 8:16], one["b4"], None, A.add), ["iu", "b4"], ["ul1"])
    V(ts(T.ident[:], T.flat[:, 0:128], one["pf"], None, A.is_equal), ["flat", "pf"], ["ident"])
    V(ts(T.dm[:], T.i16c[:], one["rf"], None, A.is_equal), ["i16c", "rf"], ["dm"])
    V(ts(T.rm[:], T.i16c[:], 1.0, None, A.min), ["i16c"], ["rm"])
    V(ts(T.ro[:], T.i20[:], one["r20"], None, A.add), ["i20", "r20"], ["ro"])

    def S(out, i, f, reads, key, **kw):
        op("s", act(out, i, f, **kw), reads, [key])

    S(T.kt[:], T.et[:, 0:720], ACT.Copy, ["etz"], "ktz")
    S(one["zf"], one["gf"], ACT.Relu, ["rf"], "zf", scale=-1.0, bias=1.0)
    S(one["h1"], one["gf"], ACT.Relu, ["rf"], "h1", bias=-3.0)
    S(one["g4"], one["gf"], ACT.Identity, ["rf"], "g4", bias=-4.0)
    S(one["e1"], one["zf"], ACT.Identity, ["zf"], "e1", scale=-1.0, bias=1.0)
    S(one["h2"], one["h1"], ACT.Sign, ["h1"], "h2")
    S(one["ef"], one["of"], ACT.Identity, ["rf", "e1"], "ef", scale=-1.0, bias=one["e1"])
    S(one["hf"], one["h2"], ACT.Identity, ["rf", "h2"], "hf", scale=8.0, bias=one["gf"])

    S(T.gt[:, 4 * C:], T.et[:, 0:128], ACT.Copy, ["etz"], "gtz")
    S(T.st[:], T.et[:, 0:600], ACT.Copy, ["etz"], "stz")

    quant("qx0", "x0", ["x0"], C)
    quant("qu", "ut", ["ut"], 128)
    ULK = ["ul0", "ul1", "ul2"]
    V(cp(T.up[:].bitcast(dt.uint32), T.qu[:].bitcast(dt.uint32).indirect(T.ul[:])), ["qu"] + ULK, ["up"])
    op("s", act(T.ups[:], T.qus[:].indirect(T.ul[:]), ACT.Copy), ["qu"] + ULK, ["ups"])
    V(ts(T.oh[:], T.jk[:], one["rf"], None, A.is_equal), ["jk", "rf"], ["oh"])
    V(tt(T.pr[:], T.oh[:], T.rw[:, 0:48], A.mult), ["oh"] + RWA, ["pr"])
    for i in range(3):
        S(T.jk[:, 16 * i:16 * i + 16], T.pr[:, 16 * i:16 * i + 16], ACT.Copy, ["pr", "oh"], "alp%d" % i, accum_out=T.al[:, i:i + 1])
    for i, (src, f) in enumerate(((0, "zf"), (0, "ef"), (1, "ef"), (2, "of"))):
        S(T.al[:, 3 + i:4 + i], T.al[:, src:src + 1], ACT.Copy, ["alp%d" % src, "rf" if f == "of" else f], "alp%d" % (3 + i), scale=one[f])
    S(T.cw[:, 0:2], T.rw[:, 58:60], ACT.Copy, RWB + ["alp4"], "cw0", scale=T.al[:, 4:5])
    S(T.cw[:, 2:4], T.rw[:, 60:62], ACT.Copy, RWB + ["alp5"], "cw1", scale=T.al[:, 5:6])
    S(T.cw[:, 4:8], T.rw[:, 51:55], ACT.Copy, RWB + ["alp6"], "cw2", scale=T.al[:, 6:7])
    for b in range(4):
        S(T.et[:, 512 * b + b:512 * (b + 1):4], T.ident[:], ACT.Copy, ["ident", "etz", "ktz", "stz", "gtz"], "et%d" % b)
    ETK = ["et%d" % b for b in range(4)]
    ETK.append("etz")

    partner = [rank ^ s for s in STEPS]

    def send(k, pairs, sem):
        dst = T.cores[partner[k]]
        rid, pid, _ = topo.addr(dst)
        eng = topo.engines(core, dst)[:8]
        m = sum(1 << e for e in eng)
        for out, in_ in pairs:
            g.remote_dma(out, in_, T.sem[sem], T.sem.lsem, pid, rid, m)
            cnt["lsem"] = cnt.get("lsem", 0) + len(eng)
            cnt[sem] = cnt.get(sem, 0) + len(eng)

    def send_state(k):
        need("g", ["qx%d" % k], [])
        send(k, [(T["rq%d" % k][:].bitcast(dt.uint8), T["qx%d" % k][:].bitcast(dt.uint8)), (T["rs%d" % k][:], T["sx%d" % k][:])], "aq%d" % k)
        done([], ["rq%d" % k], "aq%d" % k, cnt["aq%d" % k])

    def send_list(k):
        need("g", ["al%d" % k], [])
        send(k, [(T["rl%d" % k][:], T["al%d" % k][:])], "ar%d" % k)
        done([], ["rl%d" % k], "ar%d" % k, cnt["ar%d" % k])

    def signs_mm(k):
        q, s = "qx%d" % k, "sx%d" % k
        mm("b0", C, "up", "ups", 0, q, s, 0, ["up", "ups", q])
        mm("b1", C, "up", "ups", 128, q, s, 0, ["up", "ups", q])

    def signs_table():
        V(ts(T.tb1[:], T.b0[:, 0:C], 0.0, BIG, A.is_le, A.mult), ["b0"], ["tb1"])
        V(tt(T.tb[:], T.b1[:, 0:C], T.tb1[:], A.is_gt), ["b1", "tb1"], ["tb"])

    def unpack_mm(codes, scales, key):
        for b in range(4):
            mm("b%d" % (4 + b), C, "qe", "qes", 128 * b, codes, scales, 0, ["qe", key])

    def unpack_copy(dst):
        for b in range(4):
            op("s", act(T[dst][:, C * b:C * (b + 1)], T["b%d" % (4 + b)][:, 0:C], ACT.Copy), ["b%d" % (4 + b)], ["%s%d" % (dst, b)])

    send_state(0)
    signs_mm(0)

    for b in range(3):
        V(cp(T.lg[:, 7 * b:7 * b + (7 if b < 2 else 6)], T.kg32[:, b::3]), ["kg32"], ["lg0%d" % b])
    LG0 = ["lg00", "lg01", "lg02"]
    V(ts(T.pw0[:], T.pint[:].indirect(T.ro[:]), -float(HALF), None, A.add), ["pint", "ro"], ["pw0"])

    def candidates(n, k):
        src = LG0 if n == 1 else ["lg%d" % (n - 1)]
        pw = "pw%d" % (k % 2)
        V(tt(T.lm[:], T[pw][:].indirect(T.lg[:, 20 * (n - 1):20 * n]), T.dm[:], A.mult), [pw, "dm"] + src, ["lm"])
        lo, hi = C * (n - 1), C * n
        V(lambda: g.vector.tensor_tensor_scan(T.lsc[:, lo:hi], T.rm[:], T.lm[:], 0.0, A.mult, A.add), ["rm", "lm"], ["lsc%d" % n])
        V(ts(T.lg[:, 20 * n:20 * (n + 1)], T.lsc[:, lo + 15:hi:16], float(HALF), None, A.add), ["lsc%d" % n], ["lg%d" % n])

    def candidates_own(n):
        lo, hi = C * (n - 1), C * n
        for b in range(3):
            S(T.lw[:, 20 * n + b:20 * (n + 1):3], T.lsc[:, lo + 112 * b + 15:min(hi, lo + 112 * (b + 1)):16], ACT.Identity, ["lsc%d" % n], "lw%d%d" % (n, b), bias=float(HALF))

    candidates(1, 0)
    candidates_own(1)
    V(tt(T.cw[:, 8:12], T.cw[:, 0:4], T.cw[:, 4:8], A.add), ["cw0", "cw1", "cw2"], ["cw"])
    V(ts(T.gm[:, 0:84], T.bt[:], one["hf"], None, A.is_equal), ["bt", "hf"], ["gm0"])
    V(ts(T.gm[:, 88:172], T.bt[:], one["g4"], None, A.is_equal), ["bt", "g4"], ["gm1"])
    V(tt(T.cw[:, 9:10], T.cw[:, 9:10], T.al[:, 3:4], A.add), ["cw", "alp3"], ["cw"])
    for n in range(4):
        S(T.kt[:, 32 + n:32 + 4 * TW:4], T.gm[:], ACT.Copy, ["gm0", "gm1", "gmz", "cw", "ktz"], "kt%d" % n, scale=T.cw[:, 8 + n:9 + n])
    for i, (lo, f) in enumerate(((48, "of"), (55, "ef"), (62, "zf"))):
        S(T.co[:, 4 * i:4 * i + 4], T.rw[:, lo:lo + 4], ACT.Copy, RWB + ["rf" if f == "of" else f], "co%d" % i, scale=one[f])
    S(T.xc[:, 0:1], one["of"], ACT.Copy, ["rf"], "xc0", scale=14.0, bias=2.0)
    S(T.xc[:, 1:2], one["of"], ACT.Copy, ["rf"], "xc1", scale=4088.0, bias=8.0)
    candidates(2, 0)
    candidates_own(2)
    signs_table()
    candidates(3, 0)

    def gather_signs():
        for n in range(4):
            rd = ["tb"] + (LG0 if n == 0 else ["lg%d" % n])
            out, src = T.gt[:, n:4 * C:4], T.tb[:].indirect(T.lg[:, 20 * n:20 * (n + 1)])
            if n in (0, 2):
                V(cp(out, src), rd, ["gt%d" % n])
            else:
                op("s", act(out, src, ACT.Copy), rd, ["gt%d" % n])

    iota(T.tk[:], [[0, TW]], 4369, 0, [], "tka")
    op("g", lambda: g.affine_select(T.tk[:], T.tk[:], [[0, TW // 2], [1, 2]], A.not_equal, 15.0, -1, 0), ["tka"], ["tkb"])
    iota(T.tk[:, 0:84:4], [[0, 21]], 1, 0, ["tkb"], "tk")
    iota(T.mk[:], [[1, 7], [0, 12]], 0, 0, [], "mka")
    iota(T.mk[:, 80:84], [[0, 4]], -1, 0, ["mka"], "mkb")
    iota(T.rt[:], [[0, 2048]], 0, 0, [], "rtz")
    quant("qk", "kt", ["ktz"] + ["kt%d" % n for n in range(4)], 180)
    LWK = ["lw00"] + ["lw%d%d" % (n, b) for n in range(1, 4) for b in range(3)]

    def constants_a():
        quant("qe", "et", ETK, 512)
        V(ts(T.mk[:], T.mk[:], one["gf"], None, A.is_equal), ["mkb", "rf"], ["mk"])
        unpack_mm("qx0", "sx0", "qx0")

    def constants_b():
        keys = ["rtz"]
        for own in range(2):
            for gg in range(8):
                to = gg + 1 - own
                if to > 7:
                    continue
                o = 1024 * own + 512 * (gg // 4) + 64 * to + gg % 4
                keys.append("rt%d%d" % (own, gg))
                S(T.rt[:, o:o + 61:4], T.dm[:, 0:16], ACT.Copy, ["dm", "rtz"], keys[-1])
        V(tt(T.cds[:], T.co[:, 0:4], T.co[:, 4:8], A.add), ["co0", "co1"], ["cdh"])
        V(tt(T.cds[:], T.cds[:], T.co[:, 8:12], A.add), ["cdh", "co2"], ["cds"])
        quant("qr", "rt", keys, 512)

    def part(gg):
        return T.ti[:, 88 * (gg // 4) + gg % 4:88 * (gg // 4) + 84:4]

    def chain(first):
        for b in range(3):
            q = "qg" if b < 2 else "qh"
            mm("b3", TW, q, q + "s", BLK * (b % 2), "qk", "qks", 8 - 4 * b, [q, "qk"], b == 0, b == 2)
        if first:
            constants_a()
        V(tt(T.ti[:], T.b3[:, 0:TW], T.tk[:], A.add), ["b3", "tk"], ["ti"] + ["ti%d" % q for q in range(8)])
        for gg in range(1, 8):
            pd = T.pd[:, 21 * (gg - 1):21 * gg]
            V(tt(pd, part(gg), part(gg - 1), A.mult), ["ti%d" % gg, "ti%d" % (gg - 1)], ["pd%d" % gg])
            sh, mask = (3, 0x1111) if gg % 2 else (12, 15)
            V(ts(part(gg), pd, sh, mask, A.arith_shift_right, A.bitwise_and), ["pd%d" % gg], ["ti%d" % gg])
            if gg % 4 == 3:
                o = 88 * (gg // 4)
                V(tt(T.st[:, o:o + 84], T.ti[:, o:o + 84], T.mk[:], A.mult), ["mk", "stz"] + ["ti%d" % q for q in range(gg - 3, gg + 1)], ["st%d" % gg])
        if first:
            constants_b()
        quant("qs", "st", ["stz", "st3", "st7"], 150)
        if first:
            V(cp(T.lw[:, 0:20], T.kg32[:]), ["kg32"], ["lw00"])
            V(ts(T.jw[:], T.i20[:], 16.0, one["rf"], A.mult, A.add), ["i20", "rf"], ["jw"])
            V(cp(T.ml[:], T.mg32[:]), ["mg32"], ["ml"])
            V(tt(T.mj[:], T.mg32[:], T.jw[:], A.subtract), ["mg32", "jw"], ["mj"])
            unpack_copy("fo")

    def back(bank, own):
        for h in range(2):
            mm(bank, 128, "qr", "qrs", 256 * own + 128 * h, "qs", "qss", 22 * h, ["qr", "qs"], h == 0, h == 1)

    def select(k):
        for n in range(4):
            V(ts(T.ind[:, 20 * n:20 * n + 20], T.b0[:, 0:20], T.cds[:, n:n + 1], None, A.is_equal), ["b0", "cds"], ["ind%d" % n])
        V(tt(T.im[:], T.ind[:], T.lw[:], A.mult), ["ind%d" % n for n in range(4)] + LWK, ["im"])
        V(tt(T.ia[:], T.im[:, 0:40], T.im[:, 40:80], A.add), ["im"], ["ia"])
        V(tt(T.af[:], T.ia[:, 0:20], T.ia[:, 20:40], A.add), ["ia"], ["af"])
        V(cp(T["al%d" % k][:], T.af[:]), ["af"], ["al%d" % k])

    def exchange(k):
        a = "al%d" % k
        op("s", act(T.vb[:], T.sg[:].indirect(T[a][:]), ACT.Relu), ["sg", a], ["vb"])
        V(ts(T.xb[:, 0:20], T.b1[:, 0:20], T.xc[:, 0:1], None, A.is_equal), ["b1", "xc0"], ["xb0"])
        V(ts(T.xb[:, 20:40], T.b1[:, 0:20], T.xc[:, 1:2], None, A.is_equal), ["b1", "xc1"], ["xb1"])
        V(tt(T.xb[:, 40:60], T.xb[:, 0:20], T.xb[:, 20:40], A.add), ["xb0", "xb1"], ["xb2"])
        V(tt(T.ym[:], T.vb[:].indirect(T.ml[:]), T.dm[:], A.mult), ["vb", "ml", "dm"], ["ym"])
        V(lambda: g.vector.tensor_tensor_scan(T.ysc[:], T.rm[:], T.ym[:], 0.0, A.mult, A.add), ["rm", "ym"], ["ysc"])
        V(tt(T.df[:], T.ysc[:, 15::16], T.xb[:, 40:60], A.not_equal), ["ysc", "xb2"], ["df"])
        V(tt(T.sf[:, 0:20], T.df[:], T.mj[:], A.mult), ["df", "mj"], ["sf0"])
        V(tt(T.sf[:, 20:40], T.sf[:, 0:20], T.jw[:], A.add), ["sf0", "jw"], ["sf1"])
        V(cp(T.sl[:], T.sf[:, 20:40]), ["sf1"], ["sl"])
        old, new = "pw%d" % (k % 2), "pw%d" % (1 - k % 2)
        op("s", act(T[new][:], T[old][:].indirect(T.sl[:]), ACT.Copy), [old, "sl"], [new])

    for k in range(3):
        qx, sx, last = "qx%d" % k, "sx%d" % k, k == 2
        if k:
            quant(qx, "x%d" % k, ["x%d_%d" % (k, b) for b in range(4)], C)
            send_state(k)
            signs_mm(k)
            unpack_mm(qx, sx, qx)
            candidates(3, k)
            signs_table()
        mm("b2", C, "up", "ups", 256, qx, sx, 0, ["up", "ups", qx])
        gather_signs()
        candidates_own(3)
        op("s", act(T.sg[:], T.b2[:, 0:C], ACT.Sign), ["b2"], ["sg"])
        if k:
            unpack_copy("fo")
        for q, lo, hi in (("qg", 0, 240), ("qh", 224, 352)):
            V(lambda q=q, lo=lo, hi=hi: g.vector.quantize_mx(T[q][:], T[q + "s"][:], T.gt[:, 4 * lo:4 * hi]), ["gtz"] + ["gt%d" % n for n in range(4)], [q])
        chain(k == 0)
        unpack_mm("rq%d" % k, "rs%d" % k, "rq%d" % k)
        unpack_copy("fp")
        back("b0", 0)
        back("b1", 1)
        select(k)
        send_list(k)
        exchange(k)
        if not last:
            candidates(1, k + 1)
        for t in range(4):
            out, src = T.zt[:, t:4 * C:4], T.fp[:, C * t:C * (t + 1)].indirect(T["rl%d" % k][:])
            rd = ["fp%d" % t, "rl%d" % k]
            if t == 0:
                V(cp(out, src), rd, ["zt%d" % t])
            else:
                op("s", act(out, src, ACT.Copy), rd, ["zt%d" % t])
        if not last:
            candidates_own(1)
        quant("qz", "zt", ["zt%d" % t for t in range(4)], C)
        for b in range(4):
            mm("b%d" % (4 + b), C, "wq", "wqs", 128 * b, "qz", "qzs", 0, ["wq", "wqs", "qz"])
        for b in range(4):
            op("s", act(T.hs[:, C * b:C * (b + 1)], T["b%d" % (4 + b)][:, 0:C], ACT.Copy, scale=0.03125), ["b%d" % (4 + b)], ["hs%d" % b])
        if not last:
            candidates(2, k + 1)
            candidates_own(2)
        for b in range(4):
            V(tt(T["x%d" % (k + 1)][:, b::4], T.hs[:, C * b:C * (b + 1)].indirect(T["al%d" % k][:]), T.fo[:, C * b:C * (b + 1)], A.add),
              ["hs%d" % b, "al%d" % k, "fo%d" % b], ["x%d_%d" % (k + 1, b)])

    quant("qv", "vt", ["vt"], 128)
    op("s", act(T.plo[:, 0:C], T.flat[:].indirect(T.al2[:]), ACT.Copy), ["flat", "al2"], ["plo0"])
    op("s", act(T.plo[:, C:2 * C], T.pw1[:], ACT.Copy, bias=float(HALF)), ["pw1"], ["plo1"])
    quant("qx3", "x3", ["x3_%d" % b for b in range(4)], C)
    for h in range(2):
        mm("b%d" % h, C // 2, "qv", "qvs", 0, "qx3", "sx3", C // 2 * h, ["qv", "qx3"])
    dma("y", "d_op", T.pl[:], T.plo[0::16, :], ["plo0", "plo1"], [])
    dma("y", "d_oc", T.oc[:], T.qx3[:].bitcast(dt.uint8), ["qx3"], [])
    for i in range(4):
        dma("y", "d_os", T.osc[4 * i:4 * i + 4, :], T.sx3[32 * i:32 * i + 4, :], ["qx3"], [])
    V(cp(T.yo[:, 0:C // 2], T.b0[:, 0:C // 2]), ["b0"], ["yo0"])
    op("s", act(T.yo[:, C // 2:C], T.b1[:, 0:C // 2], ACT.Copy), ["b1"], ["yo1"])
    dma("s", "d_oy", T.y[:], T.yo[:], ["yo0", "yo1"], [])
    for s, v in cnt.items():
        g.wait_ge(T.sem[s], v)
